import numpy as np, ml_dtypes
CORES = [2,3,42,43,82,83,122,123]
N = 8
BF = ml_dtypes.bfloat16
B, LE, LP, M, ST, RO, TH = 1984, 160, 96, 128, 2, 3, 32768
E = RO * LE + LP
W = B + RO * ST * M
def parts(rng):
    c = (65536 * rng.random((N, 8, 16, B)) * np.exp2(-1.0 * rng.integers(0, 7, (N, 8, 1, B)))).astype(np.int64)
    return c, rng.integers(0, B, (N, 8, 16, B))
def starts(rng, c, share):
    e = np.where(rng.random((N, 8, 1, E)) < share, rng.integers(0, 3, (N, 8, 1, E)), rng.integers(4, 9, (N, 8, 1, E)))
    c[..., B - E:] = (65536 * rng.random((N, 8, 16, E)) * np.exp2(-1.0 * e)).astype(np.int64)
    return c
def pack(c, s):
    return {"c0": np.ascontiguousarray(c.reshape(N, 128, B)).astype(np.int32), "s0": np.ascontiguousarray(s.reshape(N, 128, B)).astype(np.int32)}
def setup_inputs(rng):
    c, s = parts(rng)
    return pack(starts(rng, c, rng.choice(np.array([0.4, 0.7, 0.9, 1.0]), (N, 8, 1, 1))), s)
def setup_inputs_room(rng):
    c, s = parts(rng); c = starts(rng, c, 0.8)
    for q in range(N):
        for g in range(8):
            n = int(rng.choice(np.array([0, 1, M - 1, M, M + 1, LE]))); z = int(rng.choice(np.array([0, 1, LP - 1, LP, LP + 1, M])))
            if q == 0: n = (M, M + 1, LE, M - 1, M, 1, 0, M)[g]; z = (LP, LP + 1, M, LP - 1, 0, 1, 0, 1)[g]
            live = min(n, M); z = min(z, live)
            pool = rng.permutation(B - E); ch = pool[:ST * LE].reshape(ST, LE); nil = pool[ST * LE:ST * LE + 64]; ent = B - E + np.arange(LE)
            who = np.sort(rng.permutation(LE)[:n]); drop = np.delete(who[:M], rng.permutation(live)[:z])
            c[q, g][:, ent] = 0; c[q, g][:, ent[who]] = rng.integers(30000, 65536, (16, n))
            c[q, g][:, ch.reshape(-1)] = rng.integers(20000, 65536, (16, ST * LE)); c[q, g][:, nil] = 0
            c[q, g][:, ch[ST - 1][drop]] = 0
            prev = ent
            for st in range(ST):
                own = np.where(rng.random((16, LE)) < 0.4, ch[st][None, :], rng.choice(nil, (16, LE)))
                own[rng.integers(0, 16, LE), np.arange(LE)] = ch[st]
                s[q, g][:, prev] = own; prev = ch[st]
    return pack(c, s)
def setup_inputs_ties(rng):
    c, s = parts(rng); u = TH // 16
    one = (np.arange(16).reshape(1, 1, 16, 1) == rng.integers(0, 16, (N, 8, 1, B))).astype(np.int64)
    full = rng.random((N, 8, 1, B)) < np.array([0.05, 0.1, 0.2, 0.5, 0.05, 0.1, 0.2, 0.5]).reshape(1, 8, 1, 1)
    c = np.where(full, u, u - one); c = np.where(rng.random((N, 8, 1, B)) < 0.1, 0, c)
    big = rng.random((N, 8, 1, B)) < 0.1; big[:, :4] = False; c = np.where(big, 65535, c)
    c[..., B - E:] = np.where(rng.random((N, 8, 1, E)) < 0.7, 65535, u - one[..., B - E:] * rng.integers(0, 2, (N, 8, 1, E)))
    s[:, :4] = rng.integers(0, B - E, (N, 4, 16, B))
    return pack(c, s)
def setup_inputs_alike(rng):
    c, s = parts(rng); c = starts(rng, c, 0.85)
    for q in range(N):
        for g in range(8):
            h = (1, 2, 17, 64, 160, 300, B // 4, B)[(g + q) % 8]
            s[q, g] = rng.permutation(B)[:h][rng.integers(0, h, (16, B))]
    s = np.where(rng.random(s.shape) < 0.1, np.arange(B), s)
    ends = rng.random(s.shape) < 0.05; ends[:, ::2] = False
    s = np.where(ends, rng.choice(np.array([0, B - 1]), s.shape), s); c[:, 1::2, :, 0] = 65535; c[:, 1::2, :, B - 1] = 65535
    return pack(c, s)
def setup_inputs_links(rng):
    c, s = parts(rng); c = c >> 3; c = starts(rng, c, 0.9)
    near = rng.random(s.shape) < 0.5; near[:, ::2] = True
    return pack(c, np.where(near, rng.integers(B - E, B, s.shape), s))
def setup_inputs_spread(rng):
    c, s = parts(rng); lo = rng.choice(np.array([0.0, 6.0, 10.0]), (N, 8, 1, 1))
    c = np.minimum((np.exp2(lo + (16.0 - lo) * rng.random((N, 8, 1, B))) * rng.random((N, 8, 16, B))).astype(np.int64), 65535)
    c[:, :, :, B - E::7] = rng.integers(0, 65536, c[:, :, :, B - E::7].shape)
    v = rng.random((N, 4, 16, B)); s[:, 1::2] = np.minimum((B * v * v).astype(np.int64), B - 1)
    return pack(c, s)
def check_inputs(d):
    bad = []
    for k, hi in (("c0", 65535), ("s0", B - 1)):
        if np.min(d[k]) < 0 or np.max(d[k]) > hi: bad.append("range of " + k)
    return bad
def reference(c0, s0):
    C = np.zeros((N, 8, 16, W), np.int64); S = np.zeros((N, 8, 16, W), np.int64)
    C[..., :B] = c0.reshape(N, 8, 16, B); S[..., :B] = s0.reshape(N, 8, 16, B)
    port = np.zeros((N, 8, 16, LP), np.int64)
    for rnd in range(RO):
        x = np.concatenate([B - E + rnd * LE + np.arange(LE), B - LP + np.arange(LP)])
        c = np.concatenate([C[..., x[:LE]], port], axis=3)
        for st in range(ST):
            b = B + (rnd * ST + st) * M
            sx = S[..., x]
            score = np.stack([np.add.reduce(np.minimum(c, np.take_along_axis(C, sx[:, :, i][:, :, None, :], 3)), axis=2) for i in range(16)], axis=2)
            k = np.argmax(score, axis=2); best = np.max(score, axis=2)
            y = np.take_along_axis(sx, k[:, :, None, :], 2)[:, :, 0]
            for a in range(N):
                for g in range(8):
                    l = np.flatnonzero(best[a, g] >= TH)
                    l = l[np.sort(np.unique(y[a, g, l], return_index=True)[1])][:M]
                    n = b + np.arange(l.size); yy = y[a, g, l]
                    m = np.minimum(c[a, g][:, l], C[a, g][:, yy]); old = S[a, g][:, yy]
                    C[a, g][:, yy] -= m
                    C[a, g][:, n] = m; S[a, g][:, n] = old
                    S[a, g][k[a, g, l], x[l]] = n
            x = b + np.arange(M); c = np.array(C[..., b:b + M])
        port = np.roll(c[..., :LP], 1, axis=0)
    return {"yc": C.reshape(N, 128, W).astype(np.float32), "ys": np.ascontiguousarray(S[..., B - E:]).reshape(N, 128, W - B + E).astype(np.float32)}

@@ -1,0 +1,379 @@
+from concourse.mybir import dt, AluOpType, ActivationFunctionType
+
+PAD = 136
+NV = 2752
+COL = PAD + NV
+DSZ = 368
+CW = COL + 2 * DSZ
+SW = COL + DSZ
+THR = 524287.5
+
+F32, BF, I32, U16 = "float32", "bfloat16", "int32", "uint16"
+SCRATCH = {
+    "C": ("sbuf", [128, CW], F32), "S": ("sbuf", [128, SW], F32),
+    "CL": ("sbuf", [128, 1984], I32), "SL": ("sbuf", [128, 1984], I32),
+    "S16E": ("sbuf", [128, 576], U16), "S16N": ("sbuf", [128, 128], U16),
+    "P1": ("sbuf", [128, 96], F32), "P2": ("sbuf", [128, 96], F32),
+    "CX": ("sbuf", [128, 4096], F32), "MN": ("sbuf", [128, 4096], F32),
+    "REPI": ("sbuf", [128, 64], I32), "REPL": ("sbuf", [128, 64], U16),
+    "PI": ("sbuf", [128, 1], I32), "PA": ("sbuf", [128, 1], I32), "PM": ("sbuf", [128, 1], F32),
+    "IR": ("sbuf", [128, 128], F32),
+    "ONEF": ("sbuf", [128, 128], F32), "ONEB": ("sbuf", [128, 128], BF),
+    "IDF": ("sbuf", [128, 128], F32), "ID1": ("sbuf", [128, 128], F32),
+    "IDB": ("sbuf", [128, 128], BF), "IB1": ("sbuf", [128, 128], BF),
+    "BA": ("sbuf", [128, 128], BF), "BONES": ("sbuf", [128, 128], BF),
+    "TC": ("sbuf", [128, 16], F32), "EQ": ("sbuf", [128, 16], F32),
+    "TRI": ("sbuf", [128, 2048], BF), "SEL": ("sbuf", [128, 2048], BF),
+    "SW0": ("sbuf", [128, 8], F32), "SW1": ("sbuf", [128, 8], F32), "SW16": ("sbuf", [128, 8], F32),
+    "Q0": ("sbuf", [128, 8], F32), "Q1": ("sbuf", [128, 8], F32),
+    "KB": ("sbuf", [128, 128], BF), "PB": ("sbuf", [128, 128], BF), "RST": ("sbuf", [128, 128], F32),
+    "Z3": ("sbuf", [128, 272], F32), "ZERO": ("sbuf", [128, 256], F32),
+    "DUMPY": ("sbuf", [128, 16], F32), "DUMPN": ("sbuf", [128, 96], F32),
+    "F": ("sbuf", [128, 256], F32), "EM": ("sbuf", [128, 256], F32), "AM": ("sbuf", [128, 256], F32),
+    "Y": ("sbuf", [128, 256], F32), "DE": ("sbuf", [128, 256], F32),
+    "D": ("sbuf", [128, 272], F32), "R": ("sbuf", [128, 272], F32), "WB": ("sbuf", [128, 256], BF),
+    "YO16": ("sbuf", [128, 16], U16),
+    "YU": ("sbuf", [128, 256], U16), "LV": ("sbuf", [128, 256], BF), "E": ("sbuf", [128, 4096], BF),
+    "CG": ("sbuf", [128, 256], F32), "SG": ("sbuf", [128, 256], F32),
+    "MM": ("sbuf", [128, 256], F32), "WW": ("sbuf", [128, 16], F32),
+    "DS": ("sbuf", [128, 256], F32), "RK": ("sbuf", [128, 256], BF), "DM": ("sbuf", [128, 16], F32),
+    "X": ("sbuf", [128, 32], F32), "X16": ("sbuf", [128, 32], U16),
+    "KR": ("sbuf", [128, 256], F32), "NK": ("sbuf", [128, 256], F32),
+    "KP0": ("psum", [128, 512], F32), "KP1": ("psum", [128, 512], F32), "ST": ("psum", [128, 512], F32),
+    "CON": ("psum", [128, 512], F32), "ROW": ("psum", [128, 512], F32), "DUP": ("psum", [128, 512], F32),
+    "CPB": ("psum", [128, 512], F32), "LP": ("psum", [128, 512], F32),
+}
+QUEUES = ("qv", "qs", "qt", "qp")
+DSEMS = ["dm%d" % i for i in range(12)]
+SEMAPHORES = list(QUEUES) + DSEMS + ["snd1", "snd2", "arr1", "arr2"]
+PSUM = {n for n in SCRATCH if SCRATCH[n][0] == "psum"}
+
+
+def rank_program(g, core, T, topo):
+    rank = T.rank_of(core)
+    if rank is None:
+        return
+    A, AF = AluOpType, ActivationFunctionType
+    eng = {"qv": g.vector, "qs": g.scalar, "qt": g.tensor, "qp": g, "sync": g.sync}
+    cnt, known, log, dmas = {}, {}, {}, [0]
+
+    def V(name, a=0, b=None, st=1, p=None):
+        n = SCRATCH[name][1][1]
+        b = n if b is None else b
+        t = T[name]
+        x = t[:, a:b:st] if p is None else t[p[0]:p[1], a:b:st]
+        return (x, name, a, b)
+
+    def need(q, w, r):
+        dep = {}
+        for views, wr in ((w, True), (r, False)):
+            for (_, name, a, b) in views:
+                ps = name in PSUM
+                for (lo, hi, ww, e, c) in log.get(name, ()):
+                    other = ps and e != q
+                    if not other and (hi <= a or b <= lo or not (wr or ww)):
+                        continue
+                    if ps and e == q == "qt":
+                        continue
+                    dep[e] = max(dep.get(e, 0), c)
+        for e in sorted(dep):
+            if known.get((q, e), 0) < dep[e]:
+                known[(q, e)] = dep[e]
+                eng[q].wait_ge(T.sem[e], dep[e])
+
+    def note(tok, w, r):
+        for views, wr in ((w, True), (r, False)):
+            for (_, name, a, b) in views:
+                ls = log.setdefault(name, [])
+                if wr:
+                    ls[:] = [x for x in ls if not (a <= x[0] and x[1] <= b)]
+                ls.append((a, b, wr, tok[0], tok[1]))
+
+    def op(q, fn, w, r):
+        need(q, w, r)
+        cnt[q] = cnt.get(q, 0) + 1
+        fn().then_inc(T.sem[q], 1)
+        note((q, cnt[q]), w, r)
+
+    def dma(q, out, in_, w, r):
+        need(q, w, r)
+        s = DSEMS[dmas[0]]
+        dmas[0] += 1
+        eng[q].dma_start(out, in_).then_inc(T.sem[s], 16)
+        note((s, 16), w, r)
+
+    def tt(out, a, b, o):
+        op("qv", lambda: g.vector.tensor_tensor(out[0], a[0], b[0], o), [out], [a, b])
+
+    def ts(out, a, s, o, s2=None, o2=None):
+        sc, rd = (s[0], [a, s]) if isinstance(s, tuple) else (s, [a])
+        if o2 is None:
+            op("qv", lambda: g.vector.tensor_scalar(out[0], a[0], sc, None, o), [out], rd)
+        else:
+            op("qv", lambda: g.vector.tensor_scalar(out[0], a[0], sc, s2, o, o2), [out], rd)
+
+    def cp(out, a):
+        op("qv", lambda: g.vector.tensor_copy(out[0], a[0]), [out], [a])
+
+    def scan(out, a, b, ini, o1, o2):
+        op("qv", lambda: g.vector.tensor_tensor_scan(out[0], a[0], b[0], ini, o1, o2), [out], [a, b])
+
+    def fill(out, c):
+        op("qv", lambda: g.vector.memset(out[0], c), [out], [])
+
+    def act(out, a, f=AF.Copy, **k):
+        rd = [a] + [x for x in k.values() if isinstance(x, tuple)]
+        kk = {n: (x[0] if isinstance(x, tuple) else x) for n, x in k.items()}
+        op("qs", lambda: g.scalar.activation(out[0], a[0], f, **kk), [out], rd)
+
+    def mm(out, l, r, start, stop):
+        op("qt", lambda: g.tensor.matmul(out[0], l[0], r[0], start, stop), [out], [l, r])
+
+    def iota(out, pat, base, cm):
+        op("qp", lambda: g.iota(out[0], pat, base, cm, allow_small_or_imprecise_dtypes=True), [out], [])
+
+    def asel(out, a, pat, o, base, cm):
+        op("qp", lambda: g.affine_select(out[0], a[0], pat, o, 0.0, base, cm), [out], [a])
+
+    def mix(*chains):
+        chains = [iter(c) for c in chains]
+        while chains:
+            for c in list(chains):
+                f = next(c, None)
+                if f is None:
+                    chains.remove(c)
+                else:
+                    f()
+
+    dma("sync", T.SL[:, 1408:1568], T.s0[:, 1408:1568], [V("SL", 1408, 1568)], [])
+    dma("qs", T.CL[:, 1408:1984], T.c0[:, 1408:1984], [V("CL", 1408, 1984)], [])
+    dma("sync", T.CL[:, 0:704], T.c0[:, 0:704], [V("CL", 0, 704)], [])
+    dma("qs", T.CL[:, 704:1408], T.c0[:, 704:1408], [V("CL", 704, 1408)], [])
+    dma("sync", T.SL[:, 1568:1984], T.s0[:, 1568:1984], [V("SL", 1568, 1984)], [])
+    dma("sync", T.SL[:, 0:1408], T.s0[:, 0:1408], [V("SL", 0, 1408)], [])
+
+    fill(V("ONEB"), 1.0)
+    fill(V("ONEF"), 1.0)
+    fill(V("SW0"), 16.0)
+    iota(V("REPI"), [[1, 64]], 0, 0)
+    iota(V("PI"), [[1, 1]], 0, 1)
+    iota(V("IR"), [[0, 8], [1, 16]], 0, 0)
+    asel(V("BA"), V("ONEB"), [[-16, 8], [0, 16]], A.is_ge, 0, 1)
+    asel(V("BONES"), V("BA"), [[16, 8], [0, 16]], A.is_ge, 15, -1)
+    asel(V("SW1"), V("SW0"), [[-16, 8]], A.is_ge, 0, 1)
+    asel(V("SW16"), V("SW1"), [[16, 8]], A.is_ge, 15, -1)
+    asel(V("IDF"), V("ONEF"), [[-1, 128]], A.is_equal, 0, 1)
+    iota(V("C", 128, 136), [[0, 8]], 0, 0)
+    iota(V("C", 2120, COL), [[0, 768]], 0, 0)
+    iota(V("S", 128, 136), [[0, 8]], 0, 0)
+    iota(V("S", 2120, COL), [[0, 768]], 0, 0)
+    iota(V("DUMPY"), [[16, 16]], COL + DSZ - 128, 1)
+    for u in range(6):
+        iota(V("DUMPN", 16 * u, 16 * u + 16), [[16, 16]], COL - 128 - (PAD + 1984 + 128 * u), 1)
+    cp(V("REPL"), V("REPI"))
+    ts(V("PA"), V("PI"), 15, A.bitwise_and)
+    cp(V("PM"), V("PA"))
+    ts(V("KB"), V("IR"), -1.0, A.mult, 15.0, A.add)
+    fill(V("PB"), 8.0)
+    ZMP = V("CON", 0, 128)
+    ts(ZMP, V("IR"), 0.0, A.is_gt)
+    ts(V("CON", 128, 256), V("IR"), V("PM"), A.is_equal)
+    ts(V("CON", 256, 384), V("IR"), V("PM"), A.is_equal)
+    ts(V("RST"), V("IR"), 0.0, A.is_gt, 33554432.0, A.mult)
+    ts(V("RST"), V("RST"), THR, A.max)
+    fill(V("Z3"), 1.0)
+    fill(V("Z3", 15, 272, 16), 0.0)
+    fill(V("D"), 0.0)
+    fill(V("ZERO"), 0.0)
+    ts(V("TC"), V("IR", 0, 16), V("PM"), A.is_gt)
+    ts(V("EQ"), V("IR", 0, 16), V("PM"), A.is_equal)
+
+    cp(V("S16E", 0, 160), V("SL", 1408, 1568))
+    cp(V("C", PAD + 1408, PAD + 1568), V("CL", 1408, 1568))
+    cp(V("S", PAD + 1408, PAD + 1568), V("SL", 1408, 1568))
+    cp(V("C", PAD + 1568, PAD + 1984), V("CL", 1568, 1984))
+    cp(V("C", PAD, PAD + 704), V("CL", 0, 704))
+
+    def more():
+        yield lambda: cp(V("C", PAD + 704, PAD + 1408), V("CL", 704, 1408))
+        yield lambda: cp(V("S16E", 160, 576), V("SL", 1568, 1984))
+        yield lambda: cp(V("S", PAD + 1568, PAD + 1984), V("SL", 1568, 1984))
+        yield lambda: cp(V("S", PAD, PAD + 1408), V("SL", 0, 1408))
+    late = [more]
+
+    def consts_on_scalar():
+        act(V("Q0"), V("SW16"), scale=0.0625)
+        act(V("Q1", 0, 2), V("Q0", 6, 8))
+        act(V("Q1", 2, 8), V("Q0", 0, 6))
+        act(V("ID1", 0, 32), V("IDF", 96, 128))
+        act(V("ID1", 32, 128), V("IDF", 0, 96))
+        act(V("IDB"), V("IDF"))
+        act(V("IB1"), V("ID1"))
+        for c in range(1, 16):
+            act(V("TRI", 128 * c, 128 * c + 128), V("BONES"), scale=V("TC", c, c + 1))
+        for r in range(16):
+            act(V("SEL", 128 * r, 128 * r + 128), V("IDB"), scale=V("EQ", r, r + 1))
+
+    def argmax(b):
+        o, o1, kp = 128 * b, 128 * b + 128, V("KP%d" % b, 0, 128)
+        f, em, am, y, st = (V(x, o, o1) for x in ("F", "EM", "AM", "Y", "ST"))
+        bm = V("ST", 256 + o, 256 + o1)
+        yield lambda: scan(f, V("RST"), kp, THR, A.min, A.max)
+        yield lambda: tt(em, kp, f, A.is_equal)
+        yield lambda: tt(am, ZMP, em, A.is_gt)
+        yield lambda: tt(bm, em, st, A.mult)
+        yield lambda: scan(y, am, bm, 0.0, A.mult, A.add)
+
+    def spread(bs, L):
+        o, n = 128 * bs[0], 128 * len(bs)
+        cp(V("D", o + 15, o + n, 16), V("Y", o + 15, o + n, 16))
+        scan(V("R", o + 15, o + n + 15), V("Z3", 15, n + 15), V("D", o + 15, o + n + 15), 0.0, A.mult, A.add)
+        ws = [(b, 128 * b, min(128, L - 128 * b)) for b in bs]
+        for b, p, w in ws:
+            mm(V("ROW", p, p + w), V("R", p + 15, p + 143), V(("IDF", "ID1")[b], 0, w), True, True)
+        tt(V("DE", o, o + n), V("R", o + 15, o + n + 15), V("CON", 128, 128 + n), A.mult)
+        for b, p, w in ws:
+            mm(V("LP", 8 * b, 8 * b + w // 16), V("DE", p, p + 128), V("Q%d" % b, 0, w // 16), True, True)
+
+    def step(u):
+        t, e = divmod(u, 2)
+        nb = 2 - e
+        L = (256 if t else 160) if e == 0 else 128
+        h, n0 = L // 16, 1984 + 128 * u
+        a = PAD + n0
+        ent = PAD + 1408 + 160 * t
+        ports = "P%d" % t
+        if e == 0:
+            xs = [(0, 160, ent)] + ([(160, 256, PAD + 1888)] if t else [])
+            cs = [(0, 160, "C", ent, "S16E", 160 * t)] + ([(160, 256, ports, 0, "S16E", 480)] if t else [])
+            blocks = [(0, 0, 128, 0), (128, 96, 32, 1)] + ([(160, 0, 96, 1)] if t else [])
+            chunks = [(0, 16), (16, 48), (48, 88), (88, 128), (128, 160)] + ([(160, 208), (208, 256)] if t else [])
+        else:
+            xs = [(0, 128, a - 128)]
+            cs = [(0, 128, "C", a - 128, "S16N", 0)]
+            blocks = [(0, 0, 128, 0)]
+            chunks = [(0, 32), (32, 64), (64, 96), (96, 128)]
+        for b in range(nb):
+            for (po, m, c0) in [(0, 128, xs[0][2])] if b == 0 else [(96, 32, ent + 128), (0, 96, PAD + 1888)]:
+                out = V("ST", 128 * b, 128 * b + 128, p=(po, po + m))
+                none = u == 0 and m == 96
+                mm(out, V("ONEB", 0, m, p=(0, 1)), V("PB", p=(0, 1)), True, none)
+                if not none:
+                    mm(out, V("S", c0, c0 + m), V("IDF"), False, True)
+        if u == 0:
+            mm(V("KP1", 0, 128, p=(0, 96)), V("ONEB", 0, 96, p=(0, 1)), V("KB", p=(0, 1)), True, True)
+        for (l0, l1) in chunks:
+            lo, hi, cb, cc, sb, so = [x for x in cs if x[0] <= l0 < x[1]][0]
+            src = V(cb, cc + l0 - lo, cc + l1 - lo)
+            rep, off = V("REPL", 0, l1 - l0), V(sb, so + l0 - lo, so + l1 - lo)
+            cx, mn = V("CX", 16 * l0, 16 * l1), V("MN", 16 * l0, 16 * l1)
+            op("qs", lambda: g.scalar.activation(cx[0], src[0].indirect(rep[0]), AF.Copy), [cx], [src, rep])
+            win = V("CL") if u == 0 else V("C", PAD, COL)
+            op("qv", lambda: g.vector.tensor_tensor(mn[0], win[0].indirect(off[0]), cx[0], A.min), [mn], [win, off, cx])
+            for (bl, po, m, b) in blocks:
+                if bl + m == l1:
+                    mm(V("KP%d" % b, 0, 128, p=(po, po + m)), V("ONEB", 0, m, p=(0, 1)), V("KB", p=(0, 1)), True, False)
+                    for k in range(16):
+                        mm(V("KP%d" % b, k, 128, 16, p=(po, po + m)), V("MN", 16 * bl + k, 16 * (bl + m - 1) + k + 1, 16),
+                           V("SW16"), False, k == 15)
+        ready = [f() for f in late]
+        late.clear()
+        for (lo, hi, cb, cc, sb, so) in cs:
+            act(V("CPB", lo, hi), V(cb, cc, cc + hi - lo))
+        if u == 0:
+            consts_on_scalar()
+            mix(*ready)
+            mix(argmax(0), argmax(1))
+            spread((0, 1), L)
+        elif e:
+            mix(*ready)
+            mix(argmax(0))
+            spread((0,), L)
+        else:
+            mix(*ready, argmax(0))
+            spread((0,), L)
+            mix(argmax(1))
+            spread((1,), L)
+        l3, yo = V("LP", 0, h), V("YO16", 0, h)
+        cp(V("YU", 0, L), V("ROW", 0, L))
+        cp(yo, l3)
+        lv = V("LV", 0, L)
+        act(lv, V("ROW", 0, L), AF.Sign, scale=-1.0)
+        cg, sg = V("CG", 0, L), V("SG", 0, L)
+        cwin, swin = V("C", 128, COL), V("S", 128, COL)
+        op("qs", lambda: g.scalar.activation(cg[0], cwin[0].indirect(yo[0]), AF.Copy), [cg], [cwin, yo])
+        op("qs", lambda: g.scalar.activation(sg[0], swin[0].indirect(yo[0]), AF.Copy), [sg], [swin, yo])
+        mm(V("DUP", 0, L), V("BONES"), lv, True, False)
+        for q in range(h):
+            ts(V("E", 256 * q, 256 * q + L - 16 * q), V("YU", 16 * q, L), V("LP", q, q + 1), A.is_equal)
+            if q < h - 1:
+                mm(V("DUP", 16 * q + 16, L), V("BONES"), V("E", 256 * q + 16, 256 * q + L - 16 * q), False, False)
+        for c in range(1, 16):
+            mm(V("DUP", c, L, 16), V("TRI", 128 * c, 128 * c + 128), V("E", c, 256 * (h - 1) + c + 1, 256), False, c == 15)
+        tt(V("WB", 0, 128 * nb), V("ST", 256, 256 + 128 * nb), V("R", 15, 15 + 128 * nb), A.is_equal)
+        w = V("WW", 0, h)
+        tt(w, V("DUMPY", 0, h), l3, A.subtract)
+        stn, ds, rk = V("CPB", 256, 256 + L), V("DS", 0, L), V("RK", 0, L)
+        ts(stn, V("DUP", 0, L), -16.0, A.is_equal, -1.0, A.mult)
+        scan(ds, stn, V("ZERO", 0, L), 129.0, A.add, A.max)
+        tt(rk, ds, stn, A.mult)
+        m = V("MM", 0, L)
+        tt(m, cg, V("CPB", 0, L), A.min)
+        rp = V("LP", h, 2 * h)
+        for r in range(16):
+            mm(rp, V("SEL", 128 * r, 128 * r + 128), V("RK", r, L, 16), r == 0, r == 15)
+        for b, x in enumerate((128,) if e else (128, L - 128)):
+            mm(V("ROW", 256 + 128 * b, 256 + 128 * b + x), V("WB", 128 * b, 128 * b + 128), V(("IDB", "IB1")[b], 0, x), True, True)
+        kr, kn = V("KR", 0, L), V("CPB", 256, 256 + L)
+        act(kr, rk, AF.Sign, scale=-1.0)
+        act(kn, kr, AF.Copy, scale=float(n0 + 128))
+        dm, x = V("DM", 0, h), V("X", 0, 2 * h)
+        ts(dm, rp, 0.0, A.is_equal)
+        tt(V("X", 0, h), dm, w, A.mult)
+        tt(V("X", h, 2 * h), dm, V("DUMPN", 16 * u, 16 * u + h), A.mult)
+        tt(x, x, V("LP", 0, 2 * h), A.add)
+        ts(V("X16", 0, 2 * h), x, 128.0, A.add)
+        oy, on = V("X16", 0, h), V("X16", h, 2 * h)
+        op("qv", lambda: g.vector.tensor_copy(T.C[:, a:CW].indirect(on[0]), m[0]), [V("C", a, CW)], [on, m])
+        op("qv", lambda: g.vector.tensor_tensor(T.C[:].indirect(oy[0]), cg[0], m[0], A.subtract), [V("C")], [oy, cg, m])
+        if u == 5:
+            dma("sync", T.yc[:, :], T.C[:, PAD:COL], [], [V("C", PAD, COL)])
+        op("qv", lambda: g.vector.tensor_copy(T.S[:, a:SW].indirect(on[0]), sg[0]), [V("S", a, SW)], [on, sg])
+        if e == 0:
+            cp(V("S16N"), V("S", a, a + 128))
+
+        def links():
+            yield lambda: tt(V("NK", 0, L), kn, rk, A.add)
+            yield lambda: tt(kn, V("NK", 0, L), V("ROW", 256, 256 + L), A.mult)
+            for (lo, hi, c) in xs:
+                x, y = V("S", c, c + hi - lo), V("CPB", 256 + lo, 256 + hi)
+                yield lambda: tt(x, x, y, A.max)
+            if u == 2:
+                yield lambda: cp(V("S16E", 480, 576), V("S", PAD + 1888, PAD + 1984))
+            if u == 4:
+                dma("sync", T.ys[:, 0:1088], T.S[:, PAD + 1408:PAD + 2496], [], [V("S", PAD + 1408, PAD + 2496)])
+        chain = links()
+        if e and u < 5:
+            for i in range(2):
+                next(chain)()
+        late.append(lambda: chain)
+
+        if e == 1 and t < 2:
+            nxt, prv = T.cores[(rank + 1) % len(T.cores)], T.cores[(rank - 1) % len(T.cores)]
+            rid, pid = topo.addr(nxt)[:2]
+            me, got = topo.engines(core, nxt)[:8], len(topo.engines(prv, core)[:8])
+            src, dst = V("C", a, a + 96), V("P%d" % (t + 1))
+            snd, arr = "snd%d" % (t + 1), "arr%d" % (t + 1)
+            need("qp", [], [src])
+            g.remote_dma(dst[0], src[0], T.sem[arr], T.sem[snd], pid, rid, sum(1 << i for i in me))
+            note((snd, len(me)), [], [src])
+            note((arr, got), [dst], [])
+
+    for u in range(6):
+        step(u)
+    mix(late[0]())
+    dma("sync", T.ys[:, 1088:1344], T.S[:, PAD + 2496:COL], [], [V("S", PAD + 2496, COL)])
+    for s in range(dmas[0]):
+        g.sync.wait_ge(T.sem[DSEMS[s]], 16)
+    for q in QUEUES:
+        g.sync.wait_ge(T.sem[q], cnt[q])

@@ -1,48 +1,39 @@
 from concourse.mybir import dt, AluOpType, ActivationFunctionType
 
-PAD = 136
+PAD = 256
 NV = 2752
 COL = PAD + NV
-DSZ = 368
-CW = COL + 2 * DSZ
-SW = COL + DSZ
-THR = 524287.5
+FAR = 4352
+CW = COL - 256 + FAR
+UP = 2.0 ** 60
+ON_SCALAR = ((1, 3, 4, 6, 7), range(8))
 
 F32, BF, I32, U16 = "float32", "bfloat16", "int32", "uint16"
+
+
+def sb(n, d=F32):
+    return ("sbuf", [128, n], d)
+
+
 SCRATCH = {
-    "C": ("sbuf", [128, CW], F32), "S": ("sbuf", [128, SW], F32),
-    "CL": ("sbuf", [128, 1984], I32), "SL": ("sbuf", [128, 1984], I32),
-    "S16E": ("sbuf", [128, 576], U16), "S16N": ("sbuf", [128, 128], U16),
-    "P1": ("sbuf", [128, 96], F32), "P2": ("sbuf", [128, 96], F32),
-    "CX": ("sbuf", [128, 4096], F32), "MN": ("sbuf", [128, 4096], F32),
-    "REPI": ("sbuf", [128, 64], I32), "REPL": ("sbuf", [128, 64], U16),
-    "PI": ("sbuf", [128, 1], I32), "PA": ("sbuf", [128, 1], I32), "PM": ("sbuf", [128, 1], F32),
-    "IR": ("sbuf", [128, 128], F32),
-    "ONEF": ("sbuf", [128, 128], F32), "ONEB": ("sbuf", [128, 128], BF),
-    "IDF": ("sbuf", [128, 128], F32), "ID1": ("sbuf", [128, 128], F32),
-    "IDB": ("sbuf", [128, 128], BF), "IB1": ("sbuf", [128, 128], BF),
-    "BA": ("sbuf", [128, 128], BF), "BONES": ("sbuf", [128, 128], BF),
-    "TC": ("sbuf", [128, 16], F32), "EQ": ("sbuf", [128, 16], F32),
-    "TRI": ("sbuf", [128, 2048], BF), "SEL": ("sbuf", [128, 2048], BF),
-    "SW0": ("sbuf", [128, 8], F32), "SW1": ("sbuf", [128, 8], F32), "SW16": ("sbuf", [128, 8], F32),
-    "Q0": ("sbuf", [128, 8], F32), "Q1": ("sbuf", [128, 8], F32),
-    "KB": ("sbuf", [128, 128], BF), "PB": ("sbuf", [128, 128], BF), "RST": ("sbuf", [128, 128], F32),
-    "Z3": ("sbuf", [128, 272], F32), "ZERO": ("sbuf", [128, 256], F32),
-    "DUMPY": ("sbuf", [128, 16], F32), "DUMPN": ("sbuf", [128, 96], F32),
-    "F": ("sbuf", [128, 256], F32), "EM": ("sbuf", [128, 256], F32), "AM": ("sbuf", [128, 256], F32),
-    "Y": ("sbuf", [128, 256], F32), "DE": ("sbuf", [128, 256], F32),
-    "D": ("sbuf", [128, 272], F32), "R": ("sbuf", [128, 272], F32), "WB": ("sbuf", [128, 256], BF),
-    "YO16": ("sbuf", [128, 16], U16),
-    "YU": ("sbuf", [128, 256], U16), "LV": ("sbuf", [128, 256], BF), "E": ("sbuf", [128, 4096], BF),
-    "CG": ("sbuf", [128, 256], F32), "SG": ("sbuf", [128, 256], F32),
-    "MM": ("sbuf", [128, 256], F32), "WW": ("sbuf", [128, 16], F32),
-    "DS": ("sbuf", [128, 256], F32), "RK": ("sbuf", [128, 256], BF), "DM": ("sbuf", [128, 16], F32),
-    "X": ("sbuf", [128, 32], F32), "X16": ("sbuf", [128, 32], U16),
-    "KR": ("sbuf", [128, 256], F32), "NK": ("sbuf", [128, 256], F32),
-    "KP0": ("psum", [128, 512], F32), "KP1": ("psum", [128, 512], F32), "ST": ("psum", [128, 512], F32),
-    "CON": ("psum", [128, 512], F32), "ROW": ("psum", [128, 512], F32), "DUP": ("psum", [128, 512], F32),
-    "CPB": ("psum", [128, 512], F32), "LP": ("psum", [128, 512], F32),
+    "C": sb(CW), "S": sb(CW), "CL": sb(1984, I32), "SL": sb(1984, I32),
+    "P1": sb(128), "P2": sb(128), "MN": sb(4096), "CX": sb(512),
+    "SX": sb(288), "TT": sb(544), "OKE": sb(256, U16), "OKN": sb(128, U16), "SEL": sb(16, U16), "SEL2": sb(2, U16),
+    "PI": sb(8, I32), "PF": sb(16), "TMP": sb(152), "TM2": sb(136),
+    "ONEF": sb(128), "ONEB": sb(256, BF), "ZB": sb(128, BF), "HALF": sb(128, BF), "IDF": sb(128), "ID17": sb(136),
+    "BA": sb(128, BF), "BONES": sb(128, BF), "SW0": sb(8), "SW1": sb(8), "SW16": sb(8), "Q": sb(8),
+    "KB": sb(136, BF), "PB": sb(136, BF), "Z17": sb(136), "GROW": sb(128, BF),
+    "IOTA": sb(PAD + COL), "TB": sb(144, BF), "WQ": sb(1152, BF), "POW": sb(256, BF), "WC": sb(16),
+    "L": sb(128, BF), "L2": sb(128, BF), "R": sb(128, BF), "R3": sb(16, BF), "IRB": sb(128, BF),
+    "SGN": sb(64, BF), "AB": sb(128, BF), "CR": sb(32, BF), "DUMP": sb(16), "TL": sb(128, BF),
+    "F": sb(272), "AM": sb(272), "D1": sb(272), "DE": sb(256),
+    "YB": sb(256),
+    "YO": sb(16, U16), "YF": sb(16), "YU": sb(256, U16), "DEAD": sb(256, BF), "E": ("sbuf", [128, 16, 256], BF),
+    "CG": sb(256), "SG": sb(256), "MM": sb(256), "NK": sb(256, BF), "X": sb(256, BF),
+    "ON": sb(16, U16), "OC": sb(16, U16), "OY": sb(16, U16), "T1": sb(16), "T2": sb(16), "EQ": sb(256, BF), "NR": sb(256),
 }
+for name in ("KP0", "KP1", "ST", "LP", "SUM", "CPB", "ZL", "CON"):
+    SCRATCH[name] = ("psum", [128, 512], F32)
 QUEUES = ("qv", "qs", "qt", "qp")
 DSEMS = ["dm%d" % i for i in range(12)]
 SEMAPHORES = list(QUEUES) + DSEMS + ["snd1", "snd2", "arr1", "arr2"]
@@ -63,6 +54,12 @@ def rank_program(g, core, T, topo):
         t = T[name]
         x = t[:, a:b:st] if p is None else t[p[0]:p[1], a:b:st]
         return (x, name, a, b)
+
+    def V3(name, a, b, q0=0, q1=8):
+        return (T[name][:, q0:q1, a:b], name, 0, 4096)
+
+    def VE(q, a, b):
+        return (T.E[:, q, a:b], "E", 256 * q + a, 256 * q + b)
 
     def need(q, w, r):
         dep = {}
@@ -102,38 +99,54 @@ def rank_program(g, core, T, topo):
         eng[q].dma_start(out, in_).then_inc(T.sem[s], 16)
         note((s, 16), w, r)
 
+    def ind(win, off):
+        return (win[0].indirect(off[0]),) + win[1:], off
+
+    def split(x):
+        return (x[0], [x[1]]) if len(x) == 2 else (x, [])
+
     def tt(out, a, b, o):
-        op("qv", lambda: g.vector.tensor_tensor(out[0], a[0], b[0], o), [out], [a, b])
+        (out, r0), (a, r1) = split(out), split(a)
+        op("qv", lambda: g.vector.tensor_tensor(out[0], a[0], b[0], o), [out], [a, b] + r0 + r1)
 
     def ts(out, a, s, o, s2=None, o2=None):
-        sc, rd = (s[0], [a, s]) if isinstance(s, tuple) else (s, [a])
+        rd = [a] + [x for x in (s, s2) if isinstance(x, tuple)]
+        s, s2 = (x[0] if isinstance(x, tuple) else x for x in (s, s2))
         if o2 is None:
-            op("qv", lambda: g.vector.tensor_scalar(out[0], a[0], sc, None, o), [out], rd)
+            op("qv", lambda: g.vector.tensor_scalar(out[0], a[0], s, None, o), [out], rd)
         else:
-            op("qv", lambda: g.vector.tensor_scalar(out[0], a[0], sc, s2, o, o2), [out], rd)
+            op("qv", lambda: g.vector.tensor_scalar(out[0], a[0], s, s2, o, o2), [out], rd)
 
     def cp(out, a):
-        op("qv", lambda: g.vector.tensor_copy(out[0], a[0]), [out], [a])
+        (out, r0), (a, r1) = split(out), split(a)
+        op("qv", lambda: g.vector.tensor_copy(out[0], a[0]), [out], [a] + r0 + r1)
 
     def scan(out, a, b, ini, o1, o2):
         op("qv", lambda: g.vector.tensor_tensor_scan(out[0], a[0], b[0], ini, o1, o2), [out], [a, b])
+
+    def flip(out, a):
+        op("qv", lambda: g.vector.transpose(out[0], a[0]), [out], [a])
 
     def fill(out, c):
         op("qv", lambda: g.vector.memset(out[0], c), [out], [])
 
     def act(out, a, f=AF.Copy, **k):
-        rd = [a] + [x for x in k.values() if isinstance(x, tuple)]
+        a, r1 = split(a)
+        rd = [a] + r1 + [x for x in k.values() if isinstance(x, tuple)]
         kk = {n: (x[0] if isinstance(x, tuple) else x) for n, x in k.items()}
         op("qs", lambda: g.scalar.activation(out[0], a[0], f, **kk), [out], rd)
 
     def mm(out, l, r, start, stop):
         op("qt", lambda: g.tensor.matmul(out[0], l[0], r[0], start, stop), [out], [l, r])
 
-    def iota(out, pat, base, cm):
+    def iota(out, pat, base, cm=0):
         op("qp", lambda: g.iota(out[0], pat, base, cm, allow_small_or_imprecise_dtypes=True), [out], [])
 
-    def asel(out, a, pat, o, base, cm):
-        op("qp", lambda: g.affine_select(out[0], a[0], pat, o, 0.0, base, cm), [out], [a])
+    def zero(out):
+        iota(out, [[0, out[3] - out[2]]], 0)
+
+    def asel(out, a, pat, o, base, cm, other=0.0):
+        op("qp", lambda: g.affine_select(out[0], a[0], pat, o, other, base, cm), [out], [a])
 
     def mix(*chains):
         chains = [iter(c) for c in chains]
@@ -145,224 +158,379 @@ def rank_program(g, core, T, topo):
                 else:
                     f()
 
-    dma("sync", T.SL[:, 1408:1568], T.s0[:, 1408:1568], [V("SL", 1408, 1568)], [])
-    dma("qs", T.CL[:, 1408:1984], T.c0[:, 1408:1984], [V("CL", 1408, 1984)], [])
-    dma("sync", T.CL[:, 0:704], T.c0[:, 0:704], [V("CL", 0, 704)], [])
-    dma("qs", T.CL[:, 704:1408], T.c0[:, 704:1408], [V("CL", 704, 1408)], [])
-    dma("sync", T.SL[:, 1568:1984], T.s0[:, 1568:1984], [V("SL", 1568, 1984)], [])
-    dma("sync", T.SL[:, 0:1408], T.s0[:, 0:1408], [V("SL", 0, 1408)], [])
+    row, top = (0, 1), (0, 16)
+    dma("sync", T.SL[:, 1392:1584], T.s0[:, 1392:1584], [V("SL", 1392, 1584)], [])
+    pieces = ((1216, 1984), (448, 1216), (0, 448))
+    for q, (a, b) in zip(("qs", "sync", "qs"), pieces):
+        dma(q, T.CL[:, a:b], T.c0[:, a:b], [V("CL", a, b)], [])
+    dma("sync", T.SL[:, 1584:1984], T.s0[:, 1584:1984], [V("SL", 1584, 1984)], [])
+    dma("sync", T.SL[:, 0:1392], T.s0[:, 0:1392], [V("SL", 0, 1392)], [])
 
     fill(V("ONEB"), 1.0)
     fill(V("ONEF"), 1.0)
     fill(V("SW0"), 16.0)
-    iota(V("REPI"), [[1, 64]], 0, 0)
-    iota(V("PI"), [[1, 1]], 0, 1)
-    iota(V("IR"), [[0, 8], [1, 16]], 0, 0)
-    asel(V("BA"), V("ONEB"), [[-16, 8], [0, 16]], A.is_ge, 0, 1)
-    asel(V("BONES"), V("BA"), [[16, 8], [0, 16]], A.is_ge, 15, -1)
-    asel(V("SW1"), V("SW0"), [[-16, 8]], A.is_ge, 0, 1)
-    asel(V("SW16"), V("SW1"), [[16, 8]], A.is_ge, 15, -1)
+    fill(V("TM2"), 2.0 ** -16)
+    fill(V("ZB"), 0.0)
+    fill(V("HALF"), 0.5)
+    seg = [[0, 8], [1, 16]]
+    iota(V("PI", 0, 1), [[1, 1]], 0, 1)
+    iota(V("TMP", 136, 152), [[128, 2], [2, 8]], 0)
+    iota(V("IOTA", 0, 408), [[1, 408]], -PAD)
     asel(V("IDF"), V("ONEF"), [[-1, 128]], A.is_equal, 0, 1)
-    iota(V("C", 128, 136), [[0, 8]], 0, 0)
-    iota(V("C", 2120, COL), [[0, 768]], 0, 0)
-    iota(V("S", 128, 136), [[0, 8]], 0, 0)
-    iota(V("S", 2120, COL), [[0, 768]], 0, 0)
-    iota(V("DUMPY"), [[16, 16]], COL + DSZ - 128, 1)
-    for u in range(6):
-        iota(V("DUMPN", 16 * u, 16 * u + 16), [[16, 16]], COL - 128 - (PAD + 1984 + 128 * u), 1)
-    cp(V("REPL"), V("REPI"))
-    ts(V("PA"), V("PI"), 15, A.bitwise_and)
-    cp(V("PM"), V("PA"))
-    ts(V("KB"), V("IR"), -1.0, A.mult, 15.0, A.add)
-    fill(V("PB"), 8.0)
-    ZMP = V("CON", 0, 128)
-    ts(ZMP, V("IR"), 0.0, A.is_gt)
-    ts(V("CON", 128, 256), V("IR"), V("PM"), A.is_equal)
-    ts(V("CON", 256, 384), V("IR"), V("PM"), A.is_equal)
-    ts(V("RST"), V("IR"), 0.0, A.is_gt, 33554432.0, A.mult)
-    ts(V("RST"), V("RST"), THR, A.max)
-    fill(V("Z3"), 1.0)
-    fill(V("Z3", 15, 272, 16), 0.0)
-    fill(V("D"), 0.0)
-    fill(V("ZERO"), 0.0)
-    ts(V("TC"), V("IR", 0, 16), V("PM"), A.is_gt)
-    ts(V("EQ"), V("IR", 0, 16), V("PM"), A.is_equal)
+    asel(V("BA"), V("ONEB", 0, 128), [[-16, 8], [0, 16]], A.is_ge, 0, 1)
+    asel(V("BONES"), V("BA"), [[16, 8], [0, 16]], A.is_ge, 15, -1)
+    asel(V("L", p=top), V("ONEB", 0, 128, p=top), [[0, 8], [-1, 16]], A.is_equal, 0, 1)
+    asel(V("SW1"), V("SW0"), [[-16, 8]], A.is_ge, 0, 1)
+    iota(V("KB"), [[0, 8], [-1, 17]], 16)
+    asel(V("SW16"), V("SW1"), [[16, 8]], A.is_ge, 15, -1)
+    iota(V("KB", 0, 136, 17), [[0, 8]], 524288)
+    iota(V("TMP", 0, 136), [[4096, 8], [0, 17]], PAD)
+    asel(V("ID17"), V("TM2"), [[-16, 8], [-1, 17]], A.is_equal, 1, 1)
+    iota(V("TMP", 0, 136, 17), [[4096, 8]], 0)
+    iota(V("ID17", 0, 136, 17), [[0, 8]], 0)
+    r3 = V("R3", p=top)
+    asel(r3, V("ONEB", 0, 16, p=top), [[-1, 16]], A.is_ge, 0, 1)
+    iota(V("GROW", p=row), [[-4096, 8], [0, 16]], 0)
+    asel(r3, r3, [[-1, 16]], A.not_equal, 0, 1, UP)
+    iota(V("IRB", p=row), seg, 0)
+    asel(r3, r3, [[1, 16]], A.not_equal, 0, 0, 1.0 / UP)
+    iota(V("CR", 0, 16), [[16, 16]], 0)
+    asel(r3, r3, [[1, 16]], A.not_equal, 0, 1, 1.0)
+    iota(V("SGN"), [[2, 2], [8193, 2], [0, 16]], -1)
+    iota(V("SGN", 48, 64), [[0, 16]], -8192)
+    iota(V("DUMP"), [[16, 16]], 0)
+    asel(V("R", p=top), V("ZB", p=top), [[0, 8], [-1, 16]], A.is_ge, 0, 1, -1.0)
+    iota(V("L2", p=top), [[8, 128]], 1024)
+    asel(V("L2", p=top), V("L2", p=top), [[0, 8], [-1, 16]], A.is_equal, 0, 1)
+    for b in range(2):
+        x = V("AB", 64 * b + 32, 64 * b + 64)
+        asel(x, V("SGN", 32, 64), [[0, 2], [-16, 16]], A.is_ge, 128 * b, 1)
+        asel(V("AB", 64 * b, 64 * b + 32), V("SGN", 0, 32), [[0, 2], [16, 16]], A.is_gt, -128 * b, -1)
+        asel(x, x, [[0, 2], [16, 16]], A.is_ge, 15 - 128 * b, -1)
+    iota(V("TB", 0, 128), [[1, 128]], 0)
+    iota(V("TB", 128, 144), [[0, 16]], -8192)
+    for u in (0, 2, 4):
+        zero(V("S", PAD + 1984 + 128 * u, PAD + 2128 + 128 * u))
+        zero(V("C", PAD + 1984 + 128 * u, PAD + 2112 + 128 * u))
+    for n in (408, 816):
+        act(V("IOTA", n, 2 * n), V("IOTA", 0, n), AF.Identity, bias=float(n))
+    pi = V("PI", 0, 1)
+    ts(V("PI", 1, 2), pi, 15, A.bitwise_and)
+    ts(V("PI", 2, 3), pi, 7, A.bitwise_and)
+    ts(V("PI", 3, 4), pi, 3, A.logical_shift_right, 1, A.bitwise_and)
+    ts(V("PI", 4, 5), pi, 1, A.bitwise_and)
+    ts(V("PI", 5, 6), pi, 4, A.logical_shift_right, 1, A.bitwise_and)
+    ts(V("PI", 6, 7), pi, 1, A.logical_shift_right, 7, A.bitwise_and)
+    cp(V("PF", 0, 7), V("PI", 0, 7))
+    PP, PM, P8, PH, P2, PG, PK = (V("PF", i, i + 1) for i in range(7))
+    pf = lambda i: V("PF", i, i + 1)
+    fill(V("TT", 160, 256), 0.0)
+    ts(pf(7), P2, PG, A.not_equal, 272.0, A.mult)
+    ts(pf(8), P8, 16.0, A.mult, PH, A.add)
+    ts(pf(9), P2, 16.0, A.mult, PK, A.add)
+    fill(V("YB", 0, 128), 0.0)
+    ts(V("SEL"), V("TMP", 136, 152), pf(7), A.add, pf(8), A.add)
+    ts(pf(10), pf(9), pf(7), A.add, 128.0, A.add)
+    fill(V("YB", 128, 256), 0.0)
+    ts(V("SEL2"), V("TMP", 136, 144, 4), pf(10), A.add)
+    fill(V("Z17"), 1.0)
+    fill(V("C", 0, PAD), 0.0)
+    fill(V("Z17", 0, 136, 17), 0.0)
+    scan(V("POW", 0, 128, p=row), V("HALF", p=row), V("ZB", p=row), 2.0 ** 64, A.mult, A.max)
+    fill(V("S", 0, PAD), 0.0)
+    fill(V3("E", 0, 112), 0.0)
 
-    cp(V("S16E", 0, 160), V("SL", 1408, 1568))
-    cp(V("C", PAD + 1408, PAD + 1568), V("CL", 1408, 1568))
-    cp(V("S", PAD + 1408, PAD + 1568), V("SL", 1408, 1568))
-    cp(V("C", PAD + 1568, PAD + 1984), V("CL", 1568, 1984))
-    cp(V("C", PAD, PAD + 704), V("CL", 0, 704))
+    def lists(src, n, out, sel):
+        name, a = src
+        yield lambda: flip(V("TT", 0, n), V(name, a, a + n))
+        yield lambda: flip(V("TT", 256, 256 + n + 32), V(name, a - 16, a + n + 16))
+        for o, s in zip(out, sel):
+            yield lambda: cp(o, ind(V("TT", 0, 256 + n + 32), s))
 
-    def more():
-        yield lambda: cp(V("C", PAD + 704, PAD + 1408), V("CL", 704, 1408))
-        yield lambda: cp(V("S16E", 160, 576), V("SL", 1568, 1984))
-        yield lambda: cp(V("S", PAD + 1568, PAD + 1984), V("SL", 1568, 1984))
-        yield lambda: cp(V("S", PAD, PAD + 1408), V("SL", 0, 1408))
-    late = [more]
+    cp(V("SX", 0, 192), V("SL", 1392, 1584))
+    scan(V("POW", 128, 256, p=row), V("HALF", p=row), V("L", p=row), 0.0, A.mult, A.max)
+    fill(V("HALF", 0, 1, p=row), 2.5)
+    mix(lists(("SX", 16), 160, [V("OKE", 0, 128), V("OKE", 128, 160)], [V("SEL", 0, 8), V("SEL2")]))
+    mm(V("CON", 384, 392), V("POW", 128, 256, p=row), V("POW", 0, 128, 16, p=row), True, True)
+    mm(V("CON", 392, 393), V("POW", 0, 128, p=row), V("HALF", 0, 1, p=row), True, True)
+    a, b = pieces[0]
+    cp(V("C", PAD + a, PAD + b), V("CL", a, b))
+    cp(V("WC", 0, 9), V("CON", 384, 393))
 
-    def consts_on_scalar():
-        act(V("Q0"), V("SW16"), scale=0.0625)
-        act(V("Q1", 0, 2), V("Q0", 6, 8))
-        act(V("Q1", 2, 8), V("Q0", 0, 6))
-        act(V("ID1", 0, 32), V("IDF", 96, 128))
-        act(V("ID1", 32, 128), V("IDF", 0, 96))
-        act(V("IDB"), V("IDF"))
-        act(V("IB1"), V("ID1"))
-        for c in range(1, 16):
-            act(V("TRI", 128 * c, 128 * c + 128), V("BONES"), scale=V("TC", c, c + 1))
-        for r in range(16):
-            act(V("SEL", 128 * r, 128 * r + 128), V("IDB"), scale=V("EQ", r, r + 1))
+    def twice(c):
+        for i in range(2):
+            act(V("CX", 128 * i, 128 * i + 128), V("C", c, c + 128))
 
-    def argmax(b):
-        o, o1, kp = 128 * b, 128 * b + 128, V("KP%d" % b, 0, 128)
-        f, em, am, y, st = (V(x, o, o1) for x in ("F", "EM", "AM", "Y", "ST"))
-        bm = V("ST", 256 + o, 256 + o1)
-        yield lambda: scan(f, V("RST"), kp, THR, A.min, A.max)
-        yield lambda: tt(em, kp, f, A.is_equal)
-        yield lambda: tt(am, ZMP, em, A.is_gt)
-        yield lambda: tt(bm, em, st, A.mult)
-        yield lambda: scan(y, am, bm, 0.0, A.mult, A.add)
+    act(V("CX", 256, 288), V("C", PAD + 1536, PAD + 1568))
+    twice(PAD + 1408)
+    for n in (32, 64, 128):
+        act(V("CX", 256 + n, 256 + 2 * n), V("CX", 256, 256 + n))
+    act(V("PB", p=row), V("TMP", 0, 136, p=row), scale=2.0 ** -16)
+    act(V("Q"), V("SW16"), scale=4096.0)
+    for q in range(4):
+        act(V("WQ", 128 * q, 128 * q + 128), V("BONES"), scale=V("WC", q, q + 1))
+    fill(V3("E", 128, 240, 8, 16), 0.0)
+    for a, b in pieces[1:]:
+        cp(V("C", PAD + a, PAD + b), V("CL", a, b))
 
-    def spread(bs, L):
-        o, n = 128 * bs[0], 128 * len(bs)
-        cp(V("D", o + 15, o + n, 16), V("Y", o + 15, o + n, 16))
-        scan(V("R", o + 15, o + n + 15), V("Z3", 15, n + 15), V("D", o + 15, o + n + 15), 0.0, A.mult, A.add)
-        ws = [(b, 128 * b, min(128, L - 128 * b)) for b in bs]
-        for b, p, w in ws:
-            mm(V("ROW", p, p + w), V("R", p + 15, p + 143), V(("IDF", "ID1")[b], 0, w), True, True)
-        tt(V("DE", o, o + n), V("R", o + 15, o + n + 15), V("CON", 128, 128 + n), A.mult)
-        for b, p, w in ws:
-            mm(V("LP", 8 * b, 8 * b + w // 16), V("DE", p, p + 128), V("Q%d" % b, 0, w // 16), True, True)
+    def more_consts():
+        act(V("IOTA", 1632, 3264), V("IOTA", 0, 1632), AF.Identity, bias=1632.0)
+        for q in range(4, 8):
+            act(V("WQ", 128 * q, 128 * q + 128), V("BONES"), scale=V("WC", q, q + 1))
+        act(V("WQ", 1024, 1152), V("BONES"), scale=2.0 ** 90)
+        act(V("CR", 16, 32), V("CR", 0, 16), AF.Identity, scale=-8192.0, bias=1044480.0)
+        act(V("DUMP"), V("DUMP"), AF.Identity, bias=PM)
+        for i in range(8):
+            mm(V("CON", 256 + 16 * i, 272 + 16 * i), V("L", p=top), r3, True, True)
+        for b in range(2):
+            x = V("CON", 128 * b, 128 * b + 128)
+            mm(x, V("L", p=top), V("R", p=top), True, False)
+            for i in range(b + 1):
+                mm(x, V("L2", p=top), V("L", p=top), False, i == b)
+
+    def last_consts():
+        act(V("BA"), V("BONES"), scale=-4096.0)
+        asel(V("TL"), V("BA"), [[1, 128]], A.is_gt, 0, -1)
+        asel(V("TL"), V("TL"), [[1, 128]], A.not_equal, 0, -1, 4096.0)
+
+    def close(x):
+        mm(x, V("ZB", p=row), V("ZB", 0, 8, p=row), False, True)
+
+    def payload(b, src, m=128):
+        mm(V("ST", 136 * b, 136 * b + 136), V("ONEB", 0, 128, p=row), V("PB", p=row), True, False)
+        mm(V("ST", 136 * b, 136 * b + 136, p=(0, m)), src, V("ID17"), False, m == 128)
+        if m < 128:
+            close(V("ST", 136 * b, 136 * b + 8))
+
+    def counts(b, c):
+        n = c[3] - c[2]
+        for i in range(2 if n == 128 else 1):
+            mm(V("CPB", 256 * b + 128 * i, 256 * b + 128 * i + n), V("IDF"), c, True, True)
+
+    def score_mm(b, k, m, last):
+        mm(V("KP%d" % b, 1 + k, 136, 17, p=(0, m)), V("MN", 2048 * b + m * k, 2048 * b + m * k + m), V("SW16"), False, last)
+
+    def keys(b):
+        mm(V("KP%d" % b, 0, 136), V("ONEB", 0, 128, p=row), V("KB", p=row), True, False)
+
+    def ahead(b, win, ok):
+        for j in ON_SCALAR[b]:
+            o = 2048 * b + 256 * j
+            act(V("MN", o, o + 256), ind(win, V(ok, 128 * b + 16 * j, 128 * b + 16 * j + 16)))
+
+    def scores(b, win, ok, c):
+        def own(k, n):
+            o = 2048 * b + 128 * k
+            tt(V("MN", o, o + 128 * n), ind(win, V(ok, 128 * b + 8 * k, 128 * b + 8 * (k + n))), c, A.min)
+            for i in range(k, k + n):
+                score_mm(b, i, 128, False)
+
+        def other(j):
+            x = V("MN", 2048 * b + 256 * j, 2048 * b + 256 * j + 256)
+            tt(x, x, V("CPB", 256 * b, 256 * b + 256), A.min)
+            score_mm(b, 2 * j, 128, False)
+            score_mm(b, 2 * j + 1, 128, j == 7)
+        for j in range(8):
+            if j in ON_SCALAR[b]:
+                yield lambda: other(j)
+            elif c[3] - c[2] == 256:
+                yield lambda: own(2 * j, 2)
+            else:
+                yield lambda: own(2 * j, 1)
+                yield lambda: own(2 * j + 1, 1)
+
+    def argmax(b, w=8):
+        o = 136 * b
+        kp, st = V("KP%d" % b, 0, 136), V("ST", o, o + 136)
+        f, am, d1 = (V(x, o, o + 136) for x in ("F", "AM", "D1"))
+        de, yb = (V(x, 128 * b, 128 * b + 128) for x in ("DE", "YB"))
+        yield lambda: scan(f, V("Z17"), kp, 0.0, A.mult, A.max)
+        yield lambda: tt(am, f, kp, A.is_gt)
+        yield lambda: tt(d1, st, am, A.subtract)
+        yield lambda: scan(f, am, d1, 0.0, A.mult, A.max)
+        yield lambda: cp(V("YB", 128 * b, 128 * b + 128, 16), V("F", o + 16, o + 136, 17))
+
+        def spread():
+            scan(de, yb, V("CON", 256, 384), 0.0, A.max, A.mult)
+            out = V("LP", 8 * b, 8 * b + w)
+            mm(out, V("GROW", p=row), V("ONEB", 0, w, p=row), True, False)
+            mm(out, de, V("Q", 0, w), False, True)
+        yield spread
+
+    tail, slot = [], []
+
+    def run(fs):
+        for f in fs:
+            f()
+        fs.clear()
 
     def step(u):
         t, e = divmod(u, 2)
-        nb = 2 - e
         L = (256 if t else 160) if e == 0 else 128
         h, n0 = L // 16, 1984 + 128 * u
         a = PAD + n0
         ent = PAD + 1408 + 160 * t
-        ports = "P%d" % t
-        if e == 0:
-            xs = [(0, 160, ent)] + ([(160, 256, PAD + 1888)] if t else [])
-            cs = [(0, 160, "C", ent, "S16E", 160 * t)] + ([(160, 256, ports, 0, "S16E", 480)] if t else [])
-            blocks = [(0, 0, 128, 0), (128, 96, 32, 1)] + ([(160, 0, 96, 1)] if t else [])
-            chunks = [(0, 16), (16, 48), (48, 88), (88, 128), (128, 160)] + ([(160, 208), (208, 256)] if t else [])
-        else:
-            xs = [(0, 128, a - 128)]
-            cs = [(0, 128, "C", a - 128, "S16N", 0)]
-            blocks = [(0, 0, 128, 0)]
-            chunks = [(0, 32), (32, 64), (64, 96), (96, 128)]
-        for b in range(nb):
-            for (po, m, c0) in [(0, 128, xs[0][2])] if b == 0 else [(96, 32, ent + 128), (0, 96, PAD + 1888)]:
-                out = V("ST", 128 * b, 128 * b + 128, p=(po, po + m))
-                none = u == 0 and m == 96
-                mm(out, V("ONEB", 0, m, p=(0, 1)), V("PB", p=(0, 1)), True, none)
-                if not none:
-                    mm(out, V("S", c0, c0 + m), V("IDF"), False, True)
-        if u == 0:
-            mm(V("KP1", 0, 128, p=(0, 96)), V("ONEB", 0, 96, p=(0, 1)), V("KB", p=(0, 1)), True, True)
-        for (l0, l1) in chunks:
-            lo, hi, cb, cc, sb, so = [x for x in cs if x[0] <= l0 < x[1]][0]
-            src = V(cb, cc + l0 - lo, cc + l1 - lo)
-            rep, off = V("REPL", 0, l1 - l0), V(sb, so + l0 - lo, so + l1 - lo)
-            cx, mn = V("CX", 16 * l0, 16 * l1), V("MN", 16 * l0, 16 * l1)
-            op("qs", lambda: g.scalar.activation(cx[0], src[0].indirect(rep[0]), AF.Copy), [cx], [src, rep])
-            win = V("CL") if u == 0 else V("C", PAD, COL)
-            op("qv", lambda: g.vector.tensor_tensor(mn[0], win[0].indirect(off[0]), cx[0], A.min), [mn], [win, off, cx])
-            for (bl, po, m, b) in blocks:
-                if bl + m == l1:
-                    mm(V("KP%d" % b, 0, 128, p=(po, po + m)), V("ONEB", 0, m, p=(0, 1)), V("KB", p=(0, 1)), True, False)
-                    for k in range(16):
-                        mm(V("KP%d" % b, k, 128, 16, p=(po, po + m)), V("MN", 16 * bl + k, 16 * (bl + m - 1) + k + 1, 16),
-                           V("SW16"), False, k == 15)
-        ready = [f() for f in late]
-        late.clear()
-        for (lo, hi, cb, cc, sb, so) in cs:
-            act(V("CPB", lo, hi), V(cb, cc, cc + hi - lo))
-        if u == 0:
-            consts_on_scalar()
-            mix(*ready)
-            mix(argmax(0), argmax(1))
-            spread((0, 1), L)
-        elif e:
-            mix(*ready)
+        win = V("C", PAD, a - (128 if e else 0))
+        if e:
+            keys(0)
+            ahead(0, win, "OKN")
+            mix(scores(0, win, "OKN", V("CX", 0, 256)))
+            run(tail)
             mix(argmax(0))
-            spread((0,), L)
         else:
-            mix(*ready, argmax(0))
-            spread((0,), L)
-            mix(argmax(1))
-            spread((1,), L)
-        l3, yo = V("LP", 0, h), V("YO16", 0, h)
-        cp(V("YU", 0, L), V("ROW", 0, L))
-        cp(yo, l3)
-        lv = V("LV", 0, L)
-        act(lv, V("ROW", 0, L), AF.Sign, scale=-1.0)
-        cg, sg = V("CG", 0, L), V("SG", 0, L)
-        cwin, swin = V("C", 128, COL), V("S", 128, COL)
-        op("qs", lambda: g.scalar.activation(cg[0], cwin[0].indirect(yo[0]), AF.Copy), [cg], [cwin, yo])
-        op("qs", lambda: g.scalar.activation(sg[0], swin[0].indirect(yo[0]), AF.Copy), [sg], [swin, yo])
-        mm(V("DUP", 0, L), V("BONES"), lv, True, False)
+            c0 = V("CX", 0, 256)
+            counts(0, V("C", ent, ent + 128))
+            keys(0)
+            if t:
+                c1 = V("P%d" % t)
+                ahead(0, win, "OKE")
+                act(V("P%d" % t, 0, 32), V("C", ent + 128, ent + 160))
+                ahead(1, win, "OKE")
+                mix(scores(0, win, "OKE", c0))
+                counts(1, c1)
+                keys(1)
+                run(tail)
+                mix(argmax(0), scores(1, win, "OKE", c1))
+                mix(argmax(1))
+            else:
+                payload(0, V("SX", 16, 144))
+                payload(1, V("SX", 144, 176), 32)
+                ahead(0, win, "OKE")
+                mix(scores(0, win, "OKE", c0))
+                counts(1, V("C", ent + 128, ent + 160))
+                keys(1)
+                for i in range(2):
+                    o = 2048 + 256 * i
+                    tt(V("MN", o, o + 256), ind(win, V("OKE", 128 + 16 * i, 144 + 16 * i)), V("CX", 256, 512), A.min)
+                    for k in range(8 * i, 8 * i + 8):
+                        score_mm(1, k, 32, False)
+                close(V("KP1", 0, 8))
+                more_consts()
+                mix(argmax(0), argmax(1, 2))
+                cp(V("S", PAD + 1392, PAD + 1984), V("SL", 1392, 1984))
+                cp(V("S", PAD, PAD + 1392), V("SL", 0, 1392))
+        run(slot)
+        yo, yf, yu = V("YO", 0, h), V("YF", 0, h), V("YU", 0, L)
+        cp(yo, V("LP", 0, h))
+        cp(yf, V("LP", 0, h))
+        cp(yu, ind(V("IOTA", PAD, PAD + COL), yo))
+        dead, cg, sg, m = (V(x, 0, L) for x in ("DEAD", "CG", "SG", "MM"))
+        act(dead, ind(V("IOTA", PAD, PAD + COL), yo), AF.Relu, scale=-1.0, bias=1.0)
+        act(cg, ind(V("C", 0, a), yo))
+        act(sg, ind(V("S", 0, a), yo))
+        prep = []
+        if e and t < 2:
+            act(V("SX", 0, 176), V("S", ent + 144, ent + 320))
+            act(V("SX", 176, 288), V("S", PAD + 1888, PAD + 2000))
+            prep = list(lists(("SX", 16), 256, [V("OKE")], [V("SEL")]))
+        nb = 2 - e
+        ms = [min(128, L - 128 * b) for b in range(nb)]
+        mm(V("SUM", 0, 128 * nb), V("ZB", p=row), V("ONEB", 0, 128 * nb, p=row), True, False)
+        mm(V("LP", 16, 48), V("ONEB", 0, 128, p=row), V("CR", p=row), True, False)
+        mm(V("LP", 16, 48), V("IRB", p=row), V("SGN", 32, 64, p=row), False, False)
         for q in range(h):
-            ts(V("E", 256 * q, 256 * q + L - 16 * q), V("YU", 16 * q, L), V("LP", q, q + 1), A.is_equal)
-            if q < h - 1:
-                mm(V("DUP", 16 * q + 16, L), V("BONES"), V("E", 256 * q + 16, 256 * q + L - 16 * q), False, False)
-        for c in range(1, 16):
-            mm(V("DUP", c, L, 16), V("TRI", 128 * c, 128 * c + 128), V("E", c, 256 * (h - 1) + c + 1, 256), False, c == 15)
-        tt(V("WB", 0, 128 * nb), V("ST", 256, 256 + 128 * nb), V("R", 15, 15 + 128 * nb), A.is_equal)
-        w = V("WW", 0, h)
-        tt(w, V("DUMPY", 0, h), l3, A.subtract)
-        stn, ds, rk = V("CPB", 256, 256 + L), V("DS", 0, L), V("RK", 0, L)
-        ts(stn, V("DUP", 0, L), -16.0, A.is_equal, -1.0, A.mult)
-        scan(ds, stn, V("ZERO", 0, L), 129.0, A.add, A.max)
-        tt(rk, ds, stn, A.mult)
-        m = V("MM", 0, L)
-        tt(m, cg, V("CPB", 0, L), A.min)
-        rp = V("LP", h, 2 * h)
-        for r in range(16):
-            mm(rp, V("SEL", 128 * r, 128 * r + 128), V("RK", r, L, 16), r == 0, r == 15)
-        for b, x in enumerate((128,) if e else (128, L - 128)):
-            mm(V("ROW", 256 + 128 * b, 256 + 128 * b + x), V("WB", 128 * b, 128 * b + 128), V(("IDB", "IB1")[b], 0, x), True, True)
-        kr, kn = V("KR", 0, L), V("CPB", 256, 256 + L)
-        act(kr, rk, AF.Sign, scale=-1.0)
-        act(kn, kr, AF.Copy, scale=float(n0 + 128))
-        dm, x = V("DM", 0, h), V("X", 0, 2 * h)
-        ts(dm, rp, 0.0, A.is_equal)
-        tt(V("X", 0, h), dm, w, A.mult)
-        tt(V("X", h, 2 * h), dm, V("DUMPN", 16 * u, 16 * u + h), A.mult)
-        tt(x, x, V("LP", 0, 2 * h), A.add)
-        ts(V("X16", 0, 2 * h), x, 128.0, A.add)
-        oy, on = V("X16", 0, h), V("X16", h, 2 * h)
-        op("qv", lambda: g.vector.tensor_copy(T.C[:, a:CW].indirect(on[0]), m[0]), [V("C", a, CW)], [on, m])
-        op("qv", lambda: g.vector.tensor_tensor(T.C[:].indirect(oy[0]), cg[0], m[0], A.subtract), [V("C")], [oy, cg, m])
-        if u == 5:
-            dma("sync", T.yc[:, :], T.C[:, PAD:COL], [], [V("C", PAD, COL)])
-        op("qv", lambda: g.vector.tensor_copy(T.S[:, a:SW].indirect(on[0]), sg[0]), [V("S", a, SW)], [on, sg])
-        if e == 0:
-            cp(V("S16N"), V("S", a, a + 128))
+            ts(VE(q, 16 * q, L), V("YU", 16 * q, L), V("YF", q, q + 1), A.is_equal)
+            for b in range(q // 8, nb):
+                j = q % 8 if b == q // 8 else 8
+                mm(V("SUM", 128 * b, 128 * b + 128, p=(0, ms[b])), VE(q, 128 * b, 128 * b + ms[b]),
+                   V("WQ", 128 * j, 128 * j + 128), False, q == h - 1 and u > 0)
+            if q == 3:
+                for b in range(nb):
+                    mm(V("SUM", 128 * b, 128 * b + 128, p=(0, ms[b])), V("DEAD", 128 * b, 128 * b + ms[b]),
+                       V("WQ", 1024, 1152), False, False)
+        if u == 0:
+            close(V("SUM", 0, 8))
+        tt(m, cg, V("CPB", 128, 128 + L), A.min)
+        nk, x = V("NK", 0, 128 * nb), V("X", 0, 128 * nb)
+        ts(nk, V("SUM", 0, 128 * nb), V("WC", 8, 9), A.is_ge)
+        if prep:
+            prep[0]()
+        tt(x, nk, V("CON", 0, 128 * nb), A.mult)
+        for b in range(nb):
+            mm(V("LP", 16, 48), V("NK", 128 * b, 128 * b + 128), V("AB", 64 * b, 64 * b + 32), False, False)
+        for b in range(nb):
+            mm(V("LP", 16, 48), V("X", 128 * b, 128 * b + 128), V("AB", 64 * b + 32, 64 * b + 64), False, b == nb - 1)
+        if e and t < 2:
+            payload(0, V("SX", 16, 144))
+            payload(1, V("SX", 144, 272))
+            prep[1]()
+        if u == 0:
+            last_consts()
+        sx = V("S", a - 128, a) if e else V("SX", 16, 16 + L)
+        xs = [(0, 128, a - 128)] if e else [(0, 160, ent)] + ([(160, 256, PAD + 1888)] if t else [])
 
-        def links():
-            yield lambda: tt(V("NK", 0, L), kn, rk, A.add)
-            yield lambda: tt(kn, V("NK", 0, L), V("ROW", 256, 256 + L), A.mult)
+        def same():
+            tt(V("EQ", 0, L), ind(V("IOTA", 0, COL), yo), sx, A.is_equal)
+
+        def first():
+            mm(V("ZL", 0, L), V("TL"), V("EQ", 0, L), True, False)
+            mm(V("ZL", 0, L), V("IDF"), V("NR", 0, L), False, True)
+
+        def link():
             for (lo, hi, c) in xs:
-                x, y = V("S", c, c + hi - lo), V("CPB", 256 + lo, 256 + hi)
-                yield lambda: tt(x, x, y, A.max)
-            if u == 2:
-                yield lambda: cp(V("S16E", 480, 576), V("S", PAD + 1888, PAD + 1984))
-            if u == 4:
-                dma("sync", T.ys[:, 0:1088], T.S[:, PAD + 1408:PAD + 2496], [], [V("S", PAD + 1408, PAD + 2496)])
-        chain = links()
-        if e and u < 5:
-            for i in range(2):
-                next(chain)()
-        late.append(lambda: chain)
+                y = V("S", c, c + hi - lo)
+                tt(y, y, V("ZL", lo, hi), A.max)
+        if u == 5:
+            same()
+        on, oc, oy, t1, t2 = (V(n, 0, h) for n in ("ON", "OC", "OY", "T1", "T2"))
+        far = a + (FAR if L > 128 else FAR // 2)
+        put_m = lambda: cp(ind(V("C", a, far), on), m)
+        put_s = lambda: cp(ind(V("S", a, far), on), sg)
+        put_y = lambda: tt(ind(V("C", 0, a), oy), cg, m, A.subtract)
 
-        if e == 1 and t < 2:
+        def number():
+            ts(oc, V("LP", 16, 16 + h), 128.0, A.min)
+            act(V("NR", 0, L), ind(V("TB"), oc), AF.Identity, bias=float(n0 - 4096))
+        if e == 0:
+            cp(on, V("LP", 16, 16 + h))
+            tt(t1, V("LP", 32, 32 + h), yf, A.min)
+            put_m()
+            twice(a)
+            counts(0, V("C", a, a + 128))
+            tt(t2, t1, V("DUMP", 0, h), A.max)
+            number()
+            put_s()
+            payload(0, V("S", a, a + 128))
+            f1, f2, f3 = lists(("S", a), 128, [V("OKN")], [V("SEL", 0, 8)])
+            cp(oy, t2)
+            f1()
+            f2()
+            put_y()
+            f3()
+            zero(V("S", a + 128, a + 256))
+            zero(V("C", a + 128, a + 256))
+        else:
+            tt(t1, V("LP", 32, 32 + h), yf, A.min)
+            cp(on, V("LP", 16, 16 + h))
+            tt(t2, t1, V("DUMP", 0, h), A.max)
+            number()
+            if prep:
+                prep[2]()
+            cp(oy, t2)
+            if u == 5:
+                first()
+                put_y()
+                dma("sync", T.yc[:, 0:n0], T.C[:, PAD:a], [], [V("C", PAD, a)])
+                put_m()
+                dma("qs", T.yc[:, n0:NV], T.C[:, a:COL], [], [V("C", a, COL)])
+                put_s()
+                link()
+                dma("sync", T.ys[:, 1088:1344], T.S[:, PAD + 2496:COL], [], [V("S", PAD + 2496, COL)])
+                return
+            put_y()
+            twice(ent + 160)
+            put_m()
+            slot.append(put_s)
+        tail.extend([same, first])
+        slot.append(link)
+        if u == 4:
+            slot.append(lambda: dma("sync", T.ys[:, 0:1088], T.S[:, PAD + 1408:PAD + 2496], [],
+                                    [V("S", PAD + 1408, PAD + 2496)]))
+        if e:
             nxt, prv = T.cores[(rank + 1) % len(T.cores)], T.cores[(rank - 1) % len(T.cores)]
             rid, pid = topo.addr(nxt)[:2]
             me, got = topo.engines(core, nxt)[:8], len(topo.engines(prv, core)[:8])
-            src, dst = V("C", a, a + 96), V("P%d" % (t + 1))
+            src, dst = V("C", a, a + 96), V("P%d" % (t + 1), 32, 128)
             snd, arr = "snd%d" % (t + 1), "arr%d" % (t + 1)
             need("qp", [], [src])
             g.remote_dma(dst[0], src[0], T.sem[arr], T.sem[snd], pid, rid, sum(1 << i for i in me))
@@ -371,8 +539,6 @@ def rank_program(g, core, T, topo):
 
     for u in range(6):
         step(u)
-    mix(late[0]())
-    dma("sync", T.ys[:, 1088:1344], T.S[:, PAD + 2496:COL], [], [V("S", PAD + 2496, COL)])
     for s in range(dmas[0]):
         g.sync.wait_ge(T.sem[DSEMS[s]], 16)
     for q in QUEUES:

@@ -6,6 +6,9 @@ COL = PAD + NV
 FAR = 4352
 CW = COL - 256 + FAR
 UP = 2.0 ** 60
+RATIO = 1.7
+LIFT = 32.0
+ROUND = 12582912.0
 ON_SCALAR = ((1, 3, 4, 6, 7), range(8))
 
 F32, BF, I32, U16 = "float32", "bfloat16", "int32", "uint16"
@@ -16,14 +19,14 @@ def sb(n, d=F32):
 
 
 SCRATCH = {
-    "C": sb(CW), "S": sb(CW), "CL": sb(1984, I32), "SL": sb(1984, I32),
+    "C": sb(CW), "S": sb(COL), "SS": sb(16 + FAR), "SR": sb(128), "THR": sb(256), "CL": sb(1984, I32), "SL": sb(1984, I32),
     "P1": sb(128), "P2": sb(128), "MN": sb(4096), "CX": sb(512),
     "SX": sb(288), "TT": sb(544), "OKE": sb(256, U16), "OKN": sb(128, U16), "SEL": sb(16, U16), "SEL2": sb(2, U16),
     "PI": sb(8, I32), "PF": sb(16), "TMP": sb(152), "TM2": sb(136),
-    "ONEF": sb(128), "ONEB": sb(256, BF), "ZB": sb(128, BF), "HALF": sb(128, BF), "IDF": sb(128), "ID17": sb(136),
+    "ONEF": sb(128), "ONEB": sb(256, BF), "ZB": sb(128, BF), "RHO": sb(256), "IDF": sb(128), "ID17": sb(136),
     "BA": sb(128, BF), "BONES": sb(128, BF), "SW0": sb(8), "SW1": sb(8), "SW16": sb(8), "Q": sb(8),
     "KB": sb(136, BF), "PB": sb(136, BF), "Z17": sb(136), "GROW": sb(128, BF),
-    "IOTA": sb(PAD + COL), "TB": sb(144, BF), "WQ": sb(1152, BF), "POW": sb(256, BF), "WC": sb(16),
+    "IOTA": sb(PAD + COL), "TB": sb(144, BF), "POW": sb(384), "WC": sb(18),
     "L": sb(128, BF), "L2": sb(128, BF), "R": sb(128, BF), "R3": sb(16, BF), "IRB": sb(128, BF),
     "SGN": sb(64, BF), "AB": sb(128, BF), "CR": sb(32, BF), "DUMP": sb(16), "TL": sb(128, BF),
     "F": sb(272), "AM": sb(272), "D1": sb(272), "DE": sb(256),
@@ -110,7 +113,8 @@ def rank_program(g, core, T, topo):
         op("qv", lambda: g.vector.tensor_tensor(out[0], a[0], b[0], o), [out], [a, b] + r0 + r1)
 
     def ts(out, a, s, o, s2=None, o2=None):
-        rd = [a] + [x for x in (s, s2) if isinstance(x, tuple)]
+        a, r1 = split(a)
+        rd = [a] + r1 + [x for x in (s, s2) if isinstance(x, tuple)]
         s, s2 = (x[0] if isinstance(x, tuple) else x for x in (s, s2))
         if o2 is None:
             op("qv", lambda: g.vector.tensor_scalar(out[0], a[0], s, None, o), [out], rd)
@@ -131,8 +135,8 @@ def rank_program(g, core, T, topo):
         op("qv", lambda: g.vector.memset(out[0], c), [out], [])
 
     def act(out, a, f=AF.Copy, **k):
-        a, r1 = split(a)
-        rd = [a] + r1 + [x for x in k.values() if isinstance(x, tuple)]
+        (out, r0), (a, r1) = split(out), split(a)
+        rd = [a] + r0 + r1 + [x for x in k.values() if isinstance(x, tuple)]
         kk = {n: (x[0] if isinstance(x, tuple) else x) for n, x in k.items()}
         op("qs", lambda: g.scalar.activation(out[0], a[0], f, **kk), [out], rd)
 
@@ -159,9 +163,9 @@ def rank_program(g, core, T, topo):
                     f()
 
     row, top = (0, 1), (0, 16)
-    dma("sync", T.SL[:, 1392:1584], T.s0[:, 1392:1584], [V("SL", 1392, 1584)], [])
+    dma("qs", T.SL[:, 1392:1584], T.s0[:, 1392:1584], [V("SL", 1392, 1584)], [])
     pieces = ((1216, 1984), (448, 1216), (0, 448))
-    for q, (a, b) in zip(("qs", "sync", "qs"), pieces):
+    for q, (a, b) in zip(("sync", "qs", "sync"), pieces):
         dma(q, T.CL[:, a:b], T.c0[:, a:b], [V("CL", a, b)], [])
     dma("sync", T.SL[:, 1584:1984], T.s0[:, 1584:1984], [V("SL", 1584, 1984)], [])
     dma("sync", T.SL[:, 0:1392], T.s0[:, 0:1392], [V("SL", 0, 1392)], [])
@@ -171,7 +175,7 @@ def rank_program(g, core, T, topo):
     fill(V("SW0"), 16.0)
     fill(V("TM2"), 2.0 ** -16)
     fill(V("ZB"), 0.0)
-    fill(V("HALF"), 0.5)
+    fill(V("RHO", p=row), 1.0 / RATIO)
     seg = [[0, 8], [1, 16]]
     iota(V("PI", 0, 1), [[1, 1]], 0, 1)
     iota(V("TMP", 136, 152), [[128, 2], [2, 8]], 0)
@@ -209,9 +213,13 @@ def rank_program(g, core, T, topo):
         asel(x, x, [[0, 2], [16, 16]], A.is_ge, 15 - 128 * b, -1)
     iota(V("TB", 0, 128), [[1, 128]], 0)
     iota(V("TB", 128, 144), [[0, 16]], -8192)
-    for u in (0, 2, 4):
-        zero(V("S", PAD + 1984 + 128 * u, PAD + 2128 + 128 * u))
+    iota(V("SS", 0, 160), [[0, 160]], int(LIFT))
+    zero(V("C", PAD + 1984, PAD + 2112))
+    asel(V("S", PAD, PAD + 1392), V("SL", 0, 1392), [[0, 1392]], A.is_ge, 0, 0)
+    for u in (2, 4):
         zero(V("C", PAD + 1984 + 128 * u, PAD + 2112 + 128 * u))
+    act(V("C", 0, PAD), V("ONEB"), AF.Silu, scale=0.0)
+    act(V("S", 0, PAD), V("ONEB"), scale=0.0)
     for n in (408, 816):
         act(V("IOTA", n, 2 * n), V("IOTA", 0, n), AF.Identity, bias=float(n))
     pi = V("PI", 0, 1)
@@ -234,50 +242,44 @@ def rank_program(g, core, T, topo):
     fill(V("YB", 128, 256), 0.0)
     ts(V("SEL2"), V("TMP", 136, 144, 4), pf(10), A.add)
     fill(V("Z17"), 1.0)
-    fill(V("C", 0, PAD), 0.0)
+    scan(V("POW", 0, 256, p=row), V("RHO", p=row), V("ONEB", p=row), RATIO * 2.0 ** 97, A.mult, A.mult)
     fill(V("Z17", 0, 136, 17), 0.0)
-    scan(V("POW", 0, 128, p=row), V("HALF", p=row), V("ZB", p=row), 2.0 ** 64, A.mult, A.max)
-    fill(V("S", 0, PAD), 0.0)
-    fill(V3("E", 0, 112), 0.0)
 
-    def lists(src, n, out, sel):
+    def lists(src, n, out, sel, less=0.0):
         name, a = src
         yield lambda: flip(V("TT", 0, n), V(name, a, a + n))
         yield lambda: flip(V("TT", 256, 256 + n + 32), V(name, a - 16, a + n + 16))
         for o, s in zip(out, sel):
-            yield lambda: cp(o, ind(V("TT", 0, 256 + n + 32), s))
+            yield lambda: ts(o, ind(V("TT", 0, 256 + n + 32), s), 0.25 - less, A.add)
 
     cp(V("SX", 0, 192), V("SL", 1392, 1584))
-    scan(V("POW", 128, 256, p=row), V("HALF", p=row), V("L", p=row), 0.0, A.mult, A.max)
-    fill(V("HALF", 0, 1, p=row), 2.5)
+    scan(V("POW", 256, 384, p=row), V("RHO", 0, 128, p=row), V("L", p=row), 0.0, A.mult, A.max)
+    fill(V("RHO", 0, 1, p=row), 2.56)
     mix(lists(("SX", 16), 160, [V("OKE", 0, 128), V("OKE", 128, 160)], [V("SEL", 0, 8), V("SEL2")]))
-    mm(V("CON", 384, 392), V("POW", 128, 256, p=row), V("POW", 0, 128, 16, p=row), True, True)
-    mm(V("CON", 392, 393), V("POW", 0, 128, p=row), V("HALF", 0, 1, p=row), True, True)
+    mm(V("CON", 384, 400), V("POW", 256, 384, p=row), V("POW", 0, 256, 16, p=row), True, True)
+    for b in range(2):
+        mm(V("CON", 400 + b, 401 + b), V("POW", 128 * b, 128 * b + 128, p=row), V("RHO", 0, 1, p=row), True, True)
     a, b = pieces[0]
     cp(V("C", PAD + a, PAD + b), V("CL", a, b))
-    cp(V("WC", 0, 9), V("CON", 384, 393))
+    cp(V("WC"), V("CON", 384, 402))
 
     def twice(c):
         for i in range(2):
             act(V("CX", 128 * i, 128 * i + 128), V("C", c, c + 128))
 
     act(V("CX", 256, 288), V("C", PAD + 1536, PAD + 1568))
-    twice(PAD + 1408)
+    act(V("PB", p=row), V("TMP", 0, 136, p=row), scale=2.0 ** -16)
     for n in (32, 64, 128):
         act(V("CX", 256 + n, 256 + 2 * n), V("CX", 256, 256 + n))
-    act(V("PB", p=row), V("TMP", 0, 136, p=row), scale=2.0 ** -16)
-    act(V("Q"), V("SW16"), scale=4096.0)
-    for q in range(4):
-        act(V("WQ", 128 * q, 128 * q + 128), V("BONES"), scale=V("WC", q, q + 1))
-    fill(V3("E", 128, 240, 8, 16), 0.0)
+    twice(PAD + 1408)
     for a, b in pieces[1:]:
         cp(V("C", PAD + a, PAD + b), V("CL", a, b))
 
     def more_consts():
+        act(V("Q"), V("SW16"), scale=4096.0)
         act(V("IOTA", 1632, 3264), V("IOTA", 0, 1632), AF.Identity, bias=1632.0)
-        for q in range(4, 8):
-            act(V("WQ", 128 * q, 128 * q + 128), V("BONES"), scale=V("WC", q, q + 1))
-        act(V("WQ", 1024, 1152), V("BONES"), scale=2.0 ** 90)
+        for b in range(2):
+            act(V("THR", 128 * b, 128 * b + 128), V("ONEF"), scale=V("WC", 16 + b, 17 + b))
         act(V("CR", 16, 32), V("CR", 0, 16), AF.Identity, scale=-8192.0, bias=1044480.0)
         act(V("DUMP"), V("DUMP"), AF.Identity, bias=PM)
         for i in range(8):
@@ -313,12 +315,12 @@ def rank_program(g, core, T, topo):
     def keys(b):
         mm(V("KP%d" % b, 0, 136), V("ONEB", 0, 128, p=row), V("KB", p=row), True, False)
 
-    def ahead(b, win, ok):
-        for j in ON_SCALAR[b]:
+    def ahead(b, win, ok, pairs=None):
+        for j in pairs or ON_SCALAR[b]:
             o = 2048 * b + 256 * j
             act(V("MN", o, o + 256), ind(win, V(ok, 128 * b + 16 * j, 128 * b + 16 * j + 16)))
 
-    def scores(b, win, ok, c):
+    def scores(b, win, ok, c, pairs=None):
         def own(k, n):
             o = 2048 * b + 128 * k
             tt(V("MN", o, o + 128 * n), ind(win, V(ok, 128 * b + 8 * k, 128 * b + 8 * (k + n))), c, A.min)
@@ -331,13 +333,10 @@ def rank_program(g, core, T, topo):
             score_mm(b, 2 * j, 128, False)
             score_mm(b, 2 * j + 1, 128, j == 7)
         for j in range(8):
-            if j in ON_SCALAR[b]:
+            if j in (pairs or ON_SCALAR[b]):
                 yield lambda: other(j)
-            elif c[3] - c[2] == 256:
-                yield lambda: own(2 * j, 2)
             else:
-                yield lambda: own(2 * j, 1)
-                yield lambda: own(2 * j + 1, 1)
+                yield lambda: own(2 * j, 2)
 
     def argmax(b, w=8):
         o = 136 * b
@@ -364,6 +363,13 @@ def rank_program(g, core, T, topo):
             f()
         fs.clear()
 
+    def columns(q0, q1):
+        cp(V("YO", q0, q1), V("LP", q0, q1))
+        cp(V("YF", q0, q1), V("LP", q0, q1))
+
+    def along(q0, q1):
+        cp(V("YU", 16 * q0, 16 * q1), ind(V("IOTA", PAD, PAD + COL), V("YO", q0, q1)))
+
     def step(u):
         t, e = divmod(u, 2)
         L = (256 if t else 160) if e == 0 else 128
@@ -376,7 +382,14 @@ def rank_program(g, core, T, topo):
             ahead(0, win, "OKN")
             mix(scores(0, win, "OKN", V("CX", 0, 256)))
             run(tail)
-            mix(argmax(0))
+            fs = list(argmax(0))
+            if t < 2:
+                act(V("SX", 0, 176), V("S", ent + 144, ent + 320))
+                act(V("SX", 176, 288), V("S", PAD + 1888, PAD + 2000))
+                f1, f2, f3 = lists(("SX", 16), 256, [V("OKE")], [V("SEL")])
+                fs = fs[:3] + [f1, fs[3], f2] + fs[4:] + [f3]
+            run(fs)
+            columns(0, h)
         else:
             c0 = V("CX", 0, 256)
             counts(0, V("C", ent, ent + 128))
@@ -386,65 +399,57 @@ def rank_program(g, core, T, topo):
                 ahead(0, win, "OKE")
                 act(V("P%d" % t, 0, 32), V("C", ent + 128, ent + 160))
                 ahead(1, win, "OKE")
+                run(slot)
                 mix(scores(0, win, "OKE", c0))
                 counts(1, c1)
                 keys(1)
-                run(tail)
                 mix(argmax(0), scores(1, win, "OKE", c1))
-                mix(argmax(1))
+                run(tail)
+                mix(argmax(1), [lambda: columns(0, 8), lambda: along(0, 8)])
+                columns(8, 16)
             else:
                 payload(0, V("SX", 16, 144))
                 payload(1, V("SX", 144, 176), 32)
-                ahead(0, win, "OKE")
-                mix(scores(0, win, "OKE", c0))
                 counts(1, V("C", ent + 128, ent + 160))
                 keys(1)
+                pairs = (0, 2, 3, 5, 6, 7)
+                ahead(0, win, "OKE", pairs)
                 for i in range(2):
                     o = 2048 + 256 * i
                     tt(V("MN", o, o + 256), ind(win, V("OKE", 128 + 16 * i, 144 + 16 * i)), V("CX", 256, 512), A.min)
                     for k in range(8 * i, 8 * i + 8):
                         score_mm(1, k, 32, False)
                 close(V("KP1", 0, 8))
+                mix(scores(0, win, "OKE", c0, pairs))
                 more_consts()
-                mix(argmax(0), argmax(1, 2))
-                cp(V("S", PAD + 1392, PAD + 1984), V("SL", 1392, 1984))
-                cp(V("S", PAD, PAD + 1392), V("SL", 0, 1392))
-        run(slot)
-        yo, yf, yu = V("YO", 0, h), V("YF", 0, h), V("YU", 0, L)
-        cp(yo, V("LP", 0, h))
-        cp(yf, V("LP", 0, h))
-        cp(yu, ind(V("IOTA", PAD, PAD + COL), yo))
+                cp(V("S", PAD + 1392, PAD + 1696), V("SL", 1392, 1696))
+                mix(argmax(1, 2), argmax(0))
+                cp(V("S", PAD + 1696, PAD + 1984), V("SL", 1696, 1984))
+                columns(0, h)
+        along(8 if L == 256 else 0, h)
+        yo, yf = V("YO", 0, h), V("YF", 0, h)
         dead, cg, sg, m = (V(x, 0, L) for x in ("DEAD", "CG", "SG", "MM"))
-        act(dead, ind(V("IOTA", PAD, PAD + COL), yo), AF.Relu, scale=-1.0, bias=1.0)
+        act(dead, ind(V("IOTA", PAD, PAD + COL), yo), AF.Relu, scale=-2.0 ** 99, bias=2.0 ** 99)
         act(cg, ind(V("C", 0, a), yo))
-        act(sg, ind(V("S", 0, a), yo))
-        prep = []
-        if e and t < 2:
-            act(V("SX", 0, 176), V("S", ent + 144, ent + 320))
-            act(V("SX", 176, 288), V("S", PAD + 1888, PAD + 2000))
-            prep = list(lists(("SX", 16), 256, [V("OKE")], [V("SEL")]))
+        act(sg, ind(V("S", 0, a), yo), AF.Identity, bias=LIFT)
         nb = 2 - e
         ms = [min(128, L - 128 * b) for b in range(nb)]
         mm(V("SUM", 0, 128 * nb), V("ZB", p=row), V("ONEB", 0, 128 * nb, p=row), True, False)
         mm(V("LP", 16, 48), V("ONEB", 0, 128, p=row), V("CR", p=row), True, False)
         mm(V("LP", 16, 48), V("IRB", p=row), V("SGN", 32, 64, p=row), False, False)
-        for q in range(h):
-            ts(VE(q, 16 * q, L), V("YU", 16 * q, L), V("YF", q, q + 1), A.is_equal)
-            for b in range(q // 8, nb):
-                j = q % 8 if b == q // 8 else 8
-                mm(V("SUM", 128 * b, 128 * b + 128, p=(0, ms[b])), VE(q, 128 * b, 128 * b + ms[b]),
-                   V("WQ", 128 * j, 128 * j + 128), False, q == h - 1 and u > 0)
-            if q == 3:
+        order = list(range(h - 1, -1, -1))
+        for q in order:
+            lo = 128 * (q // 8) + (0, 0, 64, 96)[q % 8 // 2]
+            ts(VE(q, lo, L), V("YU", lo, L), V("YF", q, q + 1), A.is_equal, V("WC", q, q + 1), A.mult)
+            for b in range(nb - 1, q // 8 - 1, -1):
+                p = (max(lo - 128 * b, 0), ms[b])
+                mm(V("SUM", 128 * b, 128 * b + 128, p=p), VE(q, 128 * b + p[0], 128 * b + p[1]), V("BONES"), False, q == b == 0)
+            if q == h - 4:
                 for b in range(nb):
-                    mm(V("SUM", 128 * b, 128 * b + 128, p=(0, ms[b])), V("DEAD", 128 * b, 128 * b + ms[b]),
-                       V("WQ", 1024, 1152), False, False)
-        if u == 0:
-            close(V("SUM", 0, 8))
+                    mm(V("SUM", 128 * b, 128 * b + 128, p=(0, ms[b])), V("DEAD", 128 * b, 128 * b + ms[b]), V("BONES"), False, False)
         tt(m, cg, V("CPB", 128, 128 + L), A.min)
         nk, x = V("NK", 0, 128 * nb), V("X", 0, 128 * nb)
-        ts(nk, V("SUM", 0, 128 * nb), V("WC", 8, 9), A.is_ge)
-        if prep:
-            prep[0]()
+        tt(nk, V("SUM", 0, 128 * nb), V("THR", 0, 128 * nb), A.is_ge)
         tt(x, nk, V("CON", 0, 128 * nb), A.mult)
         for b in range(nb):
             mm(V("LP", 16, 48), V("NK", 128 * b, 128 * b + 128), V("AB", 64 * b, 64 * b + 32), False, False)
@@ -453,14 +458,11 @@ def rank_program(g, core, T, topo):
         if e and t < 2:
             payload(0, V("SX", 16, 144))
             payload(1, V("SX", 144, 272))
-            prep[1]()
         if u == 0:
             last_consts()
         sx = V("S", a - 128, a) if e else V("SX", 16, 16 + L)
         xs = [(0, 128, a - 128)] if e else [(0, 160, ent)] + ([(160, 256, PAD + 1888)] if t else [])
-
-        def same():
-            tt(V("EQ", 0, L), ind(V("IOTA", 0, COL), yo), sx, A.is_equal)
+        tt(V("EQ", 0, L), ind(V("IOTA", 0, COL), yo), sx, A.is_equal)
 
         def first():
             mm(V("ZL", 0, L), V("TL"), V("EQ", 0, L), True, False)
@@ -470,61 +472,67 @@ def rank_program(g, core, T, topo):
             for (lo, hi, c) in xs:
                 y = V("S", c, c + hi - lo)
                 tt(y, y, V("ZL", lo, hi), A.max)
-        if u == 5:
-            same()
         on, oc, oy, t1, t2 = (V(n, 0, h) for n in ("ON", "OC", "OY", "T1", "T2"))
         far = a + (FAR if L > 128 else FAR // 2)
         put_m = lambda: cp(ind(V("C", a, far), on), m)
-        put_s = lambda: cp(ind(V("S", a, far), on), sg)
+        put_s = lambda: act(ind(V("SS", 16, 16 + far - a), on), sg, AF.Silu)
+
+        def settle():
+            act(V("SR"), V("SS", 16, 144), AF.Identity, bias=ROUND - LIFT)
+            act(V("S", a, a + 128), V("SR"), AF.Identity, bias=-ROUND)
+
+        def refill():
+            iota(V("SS", 0, 160), [[0, 160]], int(LIFT))
         put_y = lambda: tt(ind(V("C", 0, a), oy), cg, m, A.subtract)
 
         def number():
-            ts(oc, V("LP", 16, 16 + h), 128.0, A.min)
             act(V("NR", 0, L), ind(V("TB"), oc), AF.Identity, bias=float(n0 - 4096))
         if e == 0:
             cp(on, V("LP", 16, 16 + h))
             tt(t1, V("LP", 32, 32 + h), yf, A.min)
+            put_s()
+            ts(oc, V("LP", 16, 16 + h), 128.0, A.min)
+            tt(t2, t1, V("DUMP", 0, h), A.max)
             put_m()
             twice(a)
             counts(0, V("C", a, a + 128))
-            tt(t2, t1, V("DUMP", 0, h), A.max)
-            number()
-            put_s()
+            settle()
             payload(0, V("S", a, a + 128))
-            f1, f2, f3 = lists(("S", a), 128, [V("OKN")], [V("SEL", 0, 8)])
+            number()
+            first()
+            f1, f2, f3 = lists(("SS", 16), 128, [V("OKN")], [V("SEL", 0, 8)], LIFT)
             cp(oy, t2)
             f1()
             f2()
             put_y()
             f3()
-            zero(V("S", a + 128, a + 256))
+            refill()
             zero(V("C", a + 128, a + 256))
         else:
             tt(t1, V("LP", 32, 32 + h), yf, A.min)
             cp(on, V("LP", 16, 16 + h))
             tt(t2, t1, V("DUMP", 0, h), A.max)
-            number()
-            if prep:
-                prep[2]()
+            ts(oc, V("LP", 16, 16 + h), 128.0, A.min)
             cp(oy, t2)
+            number()
+            first()
             if u == 5:
-                first()
+                put_s()
+                settle()
                 put_y()
                 dma("sync", T.yc[:, 0:n0], T.C[:, PAD:a], [], [V("C", PAD, a)])
                 put_m()
-                dma("qs", T.yc[:, n0:NV], T.C[:, a:COL], [], [V("C", a, COL)])
-                put_s()
+                dma("sync", T.yc[:, n0:NV], T.C[:, a:COL], [], [V("C", a, COL)])
                 link()
                 dma("sync", T.ys[:, 1088:1344], T.S[:, PAD + 2496:COL], [], [V("S", PAD + 2496, COL)])
                 return
             put_y()
             twice(ent + 160)
             put_m()
-            slot.append(put_s)
-        tail.extend([same, first])
-        slot.append(link)
+            slot.extend([put_s, settle, refill])
+        tail.append(link)
         if u == 4:
-            slot.append(lambda: dma("sync", T.ys[:, 0:1088], T.S[:, PAD + 1408:PAD + 2496], [],
+            tail.append(lambda: dma("sync", T.ys[:, 0:1088], T.S[:, PAD + 1408:PAD + 2496], [],
                                     [V("S", PAD + 1408, PAD + 2496)]))
         if e:
             nxt, prv = T.cores[(rank + 1) % len(T.cores)], T.cores[(rank - 1) % len(T.cores)]

from concourse.mybir import dt, AluOpType, ActivationFunctionType

PAD = 256
NV = 2752
COL = PAD + NV
FAR = 4352
CW = COL - 256 + FAR
UP = 2.0 ** 60
RATIO = 1.7
LIFT = 32.0
ROUND = 12582912.0
ON_SCALAR = ((1, 3, 4, 6, 7), range(8))

F32, BF, I32, U16 = "float32", "bfloat16", "int32", "uint16"


def sb(n, d=F32):
    return ("sbuf", [128, n], d)


SCRATCH = {
    "C": sb(CW), "S": sb(COL), "SS": sb(16 + FAR), "SR": sb(128), "THR": sb(256), "CL": sb(1984, I32), "SL": sb(1984, I32),
    "P1": sb(128), "P2": sb(128), "MN": sb(4096), "CX": sb(512),
    "SX": sb(288), "TT": sb(544), "OKE": sb(256, U16), "OKN": sb(128, U16), "SEL": sb(16, U16), "SEL2": sb(2, U16),
    "PI": sb(8, I32), "PF": sb(16), "TMP": sb(152), "TM2": sb(136),
    "ONEF": sb(128), "ONEB": sb(256, BF), "ZB": sb(128, BF), "RHO": sb(256), "IDF": sb(128), "ID17": sb(136),
    "BA": sb(128, BF), "BONES": sb(128, BF), "SW0": sb(8), "SW1": sb(8), "SW16": sb(8), "Q": sb(8),
    "KB": sb(136, BF), "PB": sb(136, BF), "Z17": sb(136), "GROW": sb(128, BF),
    "IOTA": sb(PAD + COL), "TB": sb(144, BF), "POW": sb(384), "WC": sb(18),
    "L": sb(128, BF), "L2": sb(128, BF), "R": sb(128, BF), "R3": sb(16, BF), "IRB": sb(128, BF),
    "SGN": sb(64, BF), "AB": sb(128, BF), "CR": sb(32, BF), "DUMP": sb(16), "TL": sb(128, BF),
    "F": sb(272), "AM": sb(272), "D1": sb(272), "DE": sb(256),
    "YB": sb(256),
    "YO": sb(16, U16), "YF": sb(16), "YU": sb(256, U16), "DEAD": sb(256, BF), "E": ("sbuf", [128, 16, 256], BF),
    "CG": sb(256), "SG": sb(256), "MM": sb(256), "NK": sb(256, BF), "X": sb(256, BF),
    "ON": sb(16, U16), "OC": sb(16, U16), "OY": sb(16, U16), "T1": sb(16), "T2": sb(16), "EQ": sb(256, BF), "NR": sb(256),
}
for name in ("KP0", "KP1", "ST", "LP", "SUM", "CPB", "ZL", "CON"):
    SCRATCH[name] = ("psum", [128, 512], F32)
QUEUES = ("qv", "qs", "qt", "qp")
DSEMS = ["dm%d" % i for i in range(12)]
SEMAPHORES = list(QUEUES) + DSEMS + ["snd1", "snd2", "arr1", "arr2"]
PSUM = {n for n in SCRATCH if SCRATCH[n][0] == "psum"}


def rank_program(g, core, T, topo):
    rank = T.rank_of(core)
    if rank is None:
        return
    A, AF = AluOpType, ActivationFunctionType
    eng = {"qv": g.vector, "qs": g.scalar, "qt": g.tensor, "qp": g, "sync": g.sync}
    cnt, known, log, dmas = {}, {}, {}, [0]

    def V(name, a=0, b=None, st=1, p=None):
        n = SCRATCH[name][1][1]
        b = n if b is None else b
        t = T[name]
        x = t[:, a:b:st] if p is None else t[p[0]:p[1], a:b:st]
        return (x, name, a, b)

    def V3(name, a, b, q0=0, q1=8):
        return (T[name][:, q0:q1, a:b], name, 0, 4096)

    def VE(q, a, b):
        return (T.E[:, q, a:b], "E", 256 * q + a, 256 * q + b)

    def need(q, w, r):
        dep = {}
        for views, wr in ((w, True), (r, False)):
            for (_, name, a, b) in views:
                ps = name in PSUM
                for (lo, hi, ww, e, c) in log.get(name, ()):
                    other = ps and e != q
                    if not other and (hi <= a or b <= lo or not (wr or ww)):
                        continue
                    if ps and e == q == "qt":
                        continue
                    dep[e] = max(dep.get(e, 0), c)
        for e in sorted(dep):
            if known.get((q, e), 0) < dep[e]:
                known[(q, e)] = dep[e]
                eng[q].wait_ge(T.sem[e], dep[e])

    def note(tok, w, r):
        for views, wr in ((w, True), (r, False)):
            for (_, name, a, b) in views:
                ls = log.setdefault(name, [])
                if wr:
                    ls[:] = [x for x in ls if not (a <= x[0] and x[1] <= b)]
                ls.append((a, b, wr, tok[0], tok[1]))

    def op(q, fn, w, r):
        need(q, w, r)
        cnt[q] = cnt.get(q, 0) + 1
        fn().then_inc(T.sem[q], 1)
        note((q, cnt[q]), w, r)

    def dma(q, out, in_, w, r):
        need(q, w, r)
        s = DSEMS[dmas[0]]
        dmas[0] += 1
        eng[q].dma_start(out, in_).then_inc(T.sem[s], 16)
        note((s, 16), w, r)

    def ind(win, off):
        return (win[0].indirect(off[0]),) + win[1:], off

    def split(x):
        return (x[0], [x[1]]) if len(x) == 2 else (x, [])

    def tt(out, a, b, o):
        (out, r0), (a, r1) = split(out), split(a)
        op("qv", lambda: g.vector.tensor_tensor(out[0], a[0], b[0], o), [out], [a, b] + r0 + r1)

    def ts(out, a, s, o, s2=None, o2=None):
        a, r1 = split(a)
        rd = [a] + r1 + [x for x in (s, s2) if isinstance(x, tuple)]
        s, s2 = (x[0] if isinstance(x, tuple) else x for x in (s, s2))
        if o2 is None:
            op("qv", lambda: g.vector.tensor_scalar(out[0], a[0], s, None, o), [out], rd)
        else:
            op("qv", lambda: g.vector.tensor_scalar(out[0], a[0], s, s2, o, o2), [out], rd)

    def cp(out, a):
        (out, r0), (a, r1) = split(out), split(a)
        op("qv", lambda: g.vector.tensor_copy(out[0], a[0]), [out], [a] + r0 + r1)

    def scan(out, a, b, ini, o1, o2):
        op("qv", lambda: g.vector.tensor_tensor_scan(out[0], a[0], b[0], ini, o1, o2), [out], [a, b])

    def flip(out, a):
        op("qv", lambda: g.vector.transpose(out[0], a[0]), [out], [a])

    def fill(out, c):
        op("qv", lambda: g.vector.memset(out[0], c), [out], [])

    def act(out, a, f=AF.Copy, **k):
        (out, r0), (a, r1) = split(out), split(a)
        rd = [a] + r0 + r1 + [x for x in k.values() if isinstance(x, tuple)]
        kk = {n: (x[0] if isinstance(x, tuple) else x) for n, x in k.items()}
        op("qs", lambda: g.scalar.activation(out[0], a[0], f, **kk), [out], rd)

    def mm(out, l, r, start, stop):
        op("qt", lambda: g.tensor.matmul(out[0], l[0], r[0], start, stop), [out], [l, r])

    def iota(out, pat, base, cm=0):
        op("qp", lambda: g.iota(out[0], pat, base, cm, allow_small_or_imprecise_dtypes=True), [out], [])

    def zero(out):
        iota(out, [[0, out[3] - out[2]]], 0)

    def asel(out, a, pat, o, base, cm, other=0.0):
        op("qp", lambda: g.affine_select(out[0], a[0], pat, o, other, base, cm), [out], [a])

    def mix(*chains):
        chains = [iter(c) for c in chains]
        while chains:
            for c in list(chains):
                f = next(c, None)
                if f is None:
                    chains.remove(c)
                else:
                    f()

    row, top = (0, 1), (0, 16)
    dma("qs", T.SL[:, 1392:1584], T.s0[:, 1392:1584], [V("SL", 1392, 1584)], [])
    pieces = ((1216, 1984), (448, 1216), (0, 448))
    for q, (a, b) in zip(("sync", "qs", "sync"), pieces):
        dma(q, T.CL[:, a:b], T.c0[:, a:b], [V("CL", a, b)], [])
    dma("sync", T.SL[:, 1584:1984], T.s0[:, 1584:1984], [V("SL", 1584, 1984)], [])
    dma("sync", T.SL[:, 0:1392], T.s0[:, 0:1392], [V("SL", 0, 1392)], [])

    fill(V("ONEB"), 1.0)
    fill(V("ONEF"), 1.0)
    fill(V("SW0"), 16.0)
    fill(V("TM2"), 2.0 ** -16)
    fill(V("ZB"), 0.0)
    fill(V("RHO", p=row), 1.0 / RATIO)
    seg = [[0, 8], [1, 16]]
    iota(V("PI", 0, 1), [[1, 1]], 0, 1)
    iota(V("TMP", 136, 152), [[128, 2], [2, 8]], 0)
    iota(V("IOTA", 0, 408), [[1, 408]], -PAD)
    asel(V("IDF"), V("ONEF"), [[-1, 128]], A.is_equal, 0, 1)
    asel(V("BA"), V("ONEB", 0, 128), [[-16, 8], [0, 16]], A.is_ge, 0, 1)
    asel(V("BONES"), V("BA"), [[16, 8], [0, 16]], A.is_ge, 15, -1)
    asel(V("L", p=top), V("ONEB", 0, 128, p=top), [[0, 8], [-1, 16]], A.is_equal, 0, 1)
    asel(V("SW1"), V("SW0"), [[-16, 8]], A.is_ge, 0, 1)
    iota(V("KB"), [[0, 8], [-1, 17]], 16)
    asel(V("SW16"), V("SW1"), [[16, 8]], A.is_ge, 15, -1)
    iota(V("KB", 0, 136, 17), [[0, 8]], 524288)
    iota(V("TMP", 0, 136), [[4096, 8], [0, 17]], PAD)
    asel(V("ID17"), V("TM2"), [[-16, 8], [-1, 17]], A.is_equal, 1, 1)
    iota(V("TMP", 0, 136, 17), [[4096, 8]], 0)
    iota(V("ID17", 0, 136, 17), [[0, 8]], 0)
    r3 = V("R3", p=top)
    asel(r3, V("ONEB", 0, 16, p=top), [[-1, 16]], A.is_ge, 0, 1)
    iota(V("GROW", p=row), [[-4096, 8], [0, 16]], 0)
    asel(r3, r3, [[-1, 16]], A.not_equal, 0, 1, UP)
    iota(V("IRB", p=row), seg, 0)
    asel(r3, r3, [[1, 16]], A.not_equal, 0, 0, 1.0 / UP)
    iota(V("CR", 0, 16), [[16, 16]], 0)
    asel(r3, r3, [[1, 16]], A.not_equal, 0, 1, 1.0)
    iota(V("SGN"), [[2, 2], [8193, 2], [0, 16]], -1)
    iota(V("SGN", 48, 64), [[0, 16]], -8192)
    iota(V("DUMP"), [[16, 16]], 0)
    asel(V("R", p=top), V("ZB", p=top), [[0, 8], [-1, 16]], A.is_ge, 0, 1, -1.0)
    iota(V("L2", p=top), [[8, 128]], 1024)
    asel(V("L2", p=top), V("L2", p=top), [[0, 8], [-1, 16]], A.is_equal, 0, 1)
    for b in range(2):
        x = V("AB", 64 * b + 32, 64 * b + 64)
        asel(x, V("SGN", 32, 64), [[0, 2], [-16, 16]], A.is_ge, 128 * b, 1)
        asel(V("AB", 64 * b, 64 * b + 32), V("SGN", 0, 32), [[0, 2], [16, 16]], A.is_gt, -128 * b, -1)
        asel(x, x, [[0, 2], [16, 16]], A.is_ge, 15 - 128 * b, -1)
    iota(V("TB", 0, 128), [[1, 128]], 0)
    iota(V("TB", 128, 144), [[0, 16]], -8192)
    iota(V("SS", 0, 160), [[0, 160]], int(LIFT))
    zero(V("C", PAD + 1984, PAD + 2112))
    asel(V("S", PAD, PAD + 1392), V("SL", 0, 1392), [[0, 1392]], A.is_ge, 0, 0)
    for u in (2, 4):
        zero(V("C", PAD + 1984 + 128 * u, PAD + 2112 + 128 * u))
    act(V("C", 0, PAD), V("ONEB"), AF.Silu, scale=0.0)
    act(V("S", 0, PAD), V("ONEB"), scale=0.0)
    for n in (408, 816):
        act(V("IOTA", n, 2 * n), V("IOTA", 0, n), AF.Identity, bias=float(n))
    pi = V("PI", 0, 1)
    ts(V("PI", 1, 2), pi, 15, A.bitwise_and)
    ts(V("PI", 2, 3), pi, 7, A.bitwise_and)
    ts(V("PI", 3, 4), pi, 3, A.logical_shift_right, 1, A.bitwise_and)
    ts(V("PI", 4, 5), pi, 1, A.bitwise_and)
    ts(V("PI", 5, 6), pi, 4, A.logical_shift_right, 1, A.bitwise_and)
    ts(V("PI", 6, 7), pi, 1, A.logical_shift_right, 7, A.bitwise_and)
    cp(V("PF", 0, 7), V("PI", 0, 7))
    PP, PM, P8, PH, P2, PG, PK = (V("PF", i, i + 1) for i in range(7))
    pf = lambda i: V("PF", i, i + 1)
    fill(V("TT", 160, 256), 0.0)
    ts(pf(7), P2, PG, A.not_equal, 272.0, A.mult)
    ts(pf(8), P8, 16.0, A.mult, PH, A.add)
    ts(pf(9), P2, 16.0, A.mult, PK, A.add)
    fill(V("YB", 0, 128), 0.0)
    ts(V("SEL"), V("TMP", 136, 152), pf(7), A.add, pf(8), A.add)
    ts(pf(10), pf(9), pf(7), A.add, 128.0, A.add)
    fill(V("YB", 128, 256), 0.0)
    ts(V("SEL2"), V("TMP", 136, 144, 4), pf(10), A.add)
    fill(V("Z17"), 1.0)
    scan(V("POW", 0, 256, p=row), V("RHO", p=row), V("ONEB", p=row), RATIO * 2.0 ** 97, A.mult, A.mult)
    fill(V("Z17", 0, 136, 17), 0.0)

    def lists(src, n, out, sel, less=0.0):
        name, a = src
        yield lambda: flip(V("TT", 0, n), V(name, a, a + n))
        yield lambda: flip(V("TT", 256, 256 + n + 32), V(name, a - 16, a + n + 16))
        for o, s in zip(out, sel):
            yield lambda: ts(o, ind(V("TT", 0, 256 + n + 32), s), 0.25 - less, A.add)

    cp(V("SX", 0, 192), V("SL", 1392, 1584))
    scan(V("POW", 256, 384, p=row), V("RHO", 0, 128, p=row), V("L", p=row), 0.0, A.mult, A.max)
    fill(V("RHO", 0, 1, p=row), 2.56)
    mix(lists(("SX", 16), 160, [V("OKE", 0, 128), V("OKE", 128, 160)], [V("SEL", 0, 8), V("SEL2")]))
    mm(V("CON", 384, 400), V("POW", 256, 384, p=row), V("POW", 0, 256, 16, p=row), True, True)
    for b in range(2):
        mm(V("CON", 400 + b, 401 + b), V("POW", 128 * b, 128 * b + 128, p=row), V("RHO", 0, 1, p=row), True, True)
    a, b = pieces[0]
    cp(V("C", PAD + a, PAD + b), V("CL", a, b))
    cp(V("WC"), V("CON", 384, 402))

    def twice(c):
        for i in range(2):
            act(V("CX", 128 * i, 128 * i + 128), V("C", c, c + 128))

    act(V("CX", 256, 288), V("C", PAD + 1536, PAD + 1568))
    act(V("PB", p=row), V("TMP", 0, 136, p=row), scale=2.0 ** -16)
    for n in (32, 64, 128):
        act(V("CX", 256 + n, 256 + 2 * n), V("CX", 256, 256 + n))
    twice(PAD + 1408)
    for a, b in pieces[1:]:
        cp(V("C", PAD + a, PAD + b), V("CL", a, b))

    def more_consts():
        act(V("Q"), V("SW16"), scale=4096.0)
        act(V("IOTA", 1632, 3264), V("IOTA", 0, 1632), AF.Identity, bias=1632.0)
        for b in range(2):
            act(V("THR", 128 * b, 128 * b + 128), V("ONEF"), scale=V("WC", 16 + b, 17 + b))
        act(V("CR", 16, 32), V("CR", 0, 16), AF.Identity, scale=-8192.0, bias=1044480.0)
        act(V("DUMP"), V("DUMP"), AF.Identity, bias=PM)
        for i in range(8):
            mm(V("CON", 256 + 16 * i, 272 + 16 * i), V("L", p=top), r3, True, True)
        for b in range(2):
            x = V("CON", 128 * b, 128 * b + 128)
            mm(x, V("L", p=top), V("R", p=top), True, False)
            for i in range(b + 1):
                mm(x, V("L2", p=top), V("L", p=top), False, i == b)

    def last_consts():
        act(V("BA"), V("BONES"), scale=-4096.0)
        asel(V("TL"), V("BA"), [[1, 128]], A.is_gt, 0, -1)
        asel(V("TL"), V("TL"), [[1, 128]], A.not_equal, 0, -1, 4096.0)

    def close(x):
        mm(x, V("ZB", p=row), V("ZB", 0, 8, p=row), False, True)

    def payload(b, src, m=128):
        mm(V("ST", 136 * b, 136 * b + 136), V("ONEB", 0, 128, p=row), V("PB", p=row), True, False)
        mm(V("ST", 136 * b, 136 * b + 136, p=(0, m)), src, V("ID17"), False, m == 128)
        if m < 128:
            close(V("ST", 136 * b, 136 * b + 8))

    def counts(b, c):
        n = c[3] - c[2]
        for i in range(2 if n == 128 else 1):
            mm(V("CPB", 256 * b + 128 * i, 256 * b + 128 * i + n), V("IDF"), c, True, True)

    def score_mm(b, k, m, last):
        mm(V("KP%d" % b, 1 + k, 136, 17, p=(0, m)), V("MN", 2048 * b + m * k, 2048 * b + m * k + m), V("SW16"), False, last)

    def keys(b):
        mm(V("KP%d" % b, 0, 136), V("ONEB", 0, 128, p=row), V("KB", p=row), True, False)

    def ahead(b, win, ok, pairs=None):
        for j in pairs or ON_SCALAR[b]:
            o = 2048 * b + 256 * j
            act(V("MN", o, o + 256), ind(win, V(ok, 128 * b + 16 * j, 128 * b + 16 * j + 16)))

    def scores(b, win, ok, c, pairs=None):
        def own(k, n):
            o = 2048 * b + 128 * k
            tt(V("MN", o, o + 128 * n), ind(win, V(ok, 128 * b + 8 * k, 128 * b + 8 * (k + n))), c, A.min)
            for i in range(k, k + n):
                score_mm(b, i, 128, False)

        def other(j):
            x = V("MN", 2048 * b + 256 * j, 2048 * b + 256 * j + 256)
            tt(x, x, V("CPB", 256 * b, 256 * b + 256), A.min)
            score_mm(b, 2 * j, 128, False)
            score_mm(b, 2 * j + 1, 128, j == 7)
        for j in range(8):
            if j in (pairs or ON_SCALAR[b]):
                yield lambda: other(j)
            else:
                yield lambda: own(2 * j, 2)

    def argmax(b, w=8):
        o = 136 * b
        kp, st = V("KP%d" % b, 0, 136), V("ST", o, o + 136)
        f, am, d1 = (V(x, o, o + 136) for x in ("F", "AM", "D1"))
        de, yb = (V(x, 128 * b, 128 * b + 128) for x in ("DE", "YB"))
        yield lambda: scan(f, V("Z17"), kp, 0.0, A.mult, A.max)
        yield lambda: tt(am, f, kp, A.is_gt)
        yield lambda: tt(d1, st, am, A.subtract)
        yield lambda: scan(f, am, d1, 0.0, A.mult, A.max)
        yield lambda: cp(V("YB", 128 * b, 128 * b + 128, 16), V("F", o + 16, o + 136, 17))

        def spread():
            scan(de, yb, V("CON", 256, 384), 0.0, A.max, A.mult)
            out = V("LP", 8 * b, 8 * b + w)
            mm(out, V("GROW", p=row), V("ONEB", 0, w, p=row), True, False)
            mm(out, de, V("Q", 0, w), False, True)
        yield spread

    tail, slot = [], []

    def run(fs):
        for f in fs:
            f()
        fs.clear()

    def columns(q0, q1):
        cp(V("YO", q0, q1), V("LP", q0, q1))
        cp(V("YF", q0, q1), V("LP", q0, q1))

    def along(q0, q1):
        cp(V("YU", 16 * q0, 16 * q1), ind(V("IOTA", PAD, PAD + COL), V("YO", q0, q1)))

    def step(u):
        t, e = divmod(u, 2)
        L = (256 if t else 160) if e == 0 else 128
        h, n0 = L // 16, 1984 + 128 * u
        a = PAD + n0
        ent = PAD + 1408 + 160 * t
        win = V("C", PAD, a - (128 if e else 0))
        if e:
            keys(0)
            ahead(0, win, "OKN")
            mix(scores(0, win, "OKN", V("CX", 0, 256)))
            run(tail)
            fs = list(argmax(0))
            if t < 2:
                act(V("SX", 0, 176), V("S", ent + 144, ent + 320))
                act(V("SX", 176, 288), V("S", PAD + 1888, PAD + 2000))
                f1, f2, f3 = lists(("SX", 16), 256, [V("OKE")], [V("SEL")])
                fs = fs[:3] + [f1, fs[3], f2] + fs[4:] + [f3]
            run(fs)
            columns(0, h)
        else:
            c0 = V("CX", 0, 256)
            counts(0, V("C", ent, ent + 128))
            keys(0)
            if t:
                c1 = V("P%d" % t)
                ahead(0, win, "OKE")
                act(V("P%d" % t, 0, 32), V("C", ent + 128, ent + 160))
                ahead(1, win, "OKE")
                run(slot)
                mix(scores(0, win, "OKE", c0))
                counts(1, c1)
                keys(1)
                mix(argmax(0), scores(1, win, "OKE", c1))
                run(tail)
                mix(argmax(1), [lambda: columns(0, 8), lambda: along(0, 8)])
                columns(8, 16)
            else:
                payload(0, V("SX", 16, 144))
                payload(1, V("SX", 144, 176), 32)
                counts(1, V("C", ent + 128, ent + 160))
                keys(1)
                pairs = (0, 2, 3, 5, 6, 7)
                ahead(0, win, "OKE", pairs)
                for i in range(2):
                    o = 2048 + 256 * i
                    tt(V("MN", o, o + 256), ind(win, V("OKE", 128 + 16 * i, 144 + 16 * i)), V("CX", 256, 512), A.min)
                    for k in range(8 * i, 8 * i + 8):
                        score_mm(1, k, 32, False)
                close(V("KP1", 0, 8))
                mix(scores(0, win, "OKE", c0, pairs))
                more_consts()
                cp(V("S", PAD + 1392, PAD + 1696), V("SL", 1392, 1696))
                mix(argmax(1, 2), argmax(0))
                cp(V("S", PAD + 1696, PAD + 1984), V("SL", 1696, 1984))
                columns(0, h)
        along(8 if L == 256 else 0, h)
        yo, yf = V("YO", 0, h), V("YF", 0, h)
        dead, cg, sg, m = (V(x, 0, L) for x in ("DEAD", "CG", "SG", "MM"))
        act(dead, ind(V("IOTA", PAD, PAD + COL), yo), AF.Relu, scale=-2.0 ** 99, bias=2.0 ** 99)
        act(cg, ind(V("C", 0, a), yo))
        act(sg, ind(V("S", 0, a), yo), AF.Identity, bias=LIFT)
        nb = 2 - e
        ms = [min(128, L - 128 * b) for b in range(nb)]
        mm(V("SUM", 0, 128 * nb), V("ZB", p=row), V("ONEB", 0, 128 * nb, p=row), True, False)
        mm(V("LP", 16, 48), V("ONEB", 0, 128, p=row), V("CR", p=row), True, False)
        mm(V("LP", 16, 48), V("IRB", p=row), V("SGN", 32, 64, p=row), False, False)
        order = list(range(h - 1, -1, -1))
        for q in order:
            lo = 128 * (q // 8) + (0, 0, 64, 96)[q % 8 // 2]
            ts(VE(q, lo, L), V("YU", lo, L), V("YF", q, q + 1), A.is_equal, V("WC", q, q + 1), A.mult)
            for b in range(nb - 1, q // 8 - 1, -1):
                p = (max(lo - 128 * b, 0), ms[b])
                mm(V("SUM", 128 * b, 128 * b + 128, p=p), VE(q, 128 * b + p[0], 128 * b + p[1]), V("BONES"), False, q == b == 0)
            if q == h - 4:
                for b in range(nb):
                    mm(V("SUM", 128 * b, 128 * b + 128, p=(0, ms[b])), V("DEAD", 128 * b, 128 * b + ms[b]), V("BONES"), False, False)
        tt(m, cg, V("CPB", 128, 128 + L), A.min)
        nk, x = V("NK", 0, 128 * nb), V("X", 0, 128 * nb)
        tt(nk, V("SUM", 0, 128 * nb), V("THR", 0, 128 * nb), A.is_ge)
        tt(x, nk, V("CON", 0, 128 * nb), A.mult)
        for b in range(nb):
            mm(V("LP", 16, 48), V("NK", 128 * b, 128 * b + 128), V("AB", 64 * b, 64 * b + 32), False, False)
        for b in range(nb):
            mm(V("LP", 16, 48), V("X", 128 * b, 128 * b + 128), V("AB", 64 * b + 32, 64 * b + 64), False, b == nb - 1)
        if e and t < 2:
            payload(0, V("SX", 16, 144))
            payload(1, V("SX", 144, 272))
        if u == 0:
            last_consts()
        sx = V("S", a - 128, a) if e else V("SX", 16, 16 + L)
        xs = [(0, 128, a - 128)] if e else [(0, 160, ent)] + ([(160, 256, PAD + 1888)] if t else [])
        tt(V("EQ", 0, L), ind(V("IOTA", 0, COL), yo), sx, A.is_equal)

        def first():
            mm(V("ZL", 0, L), V("TL"), V("EQ", 0, L), True, False)
            mm(V("ZL", 0, L), V("IDF"), V("NR", 0, L), False, True)

        def link():
            for (lo, hi, c) in xs:
                y = V("S", c, c + hi - lo)
                tt(y, y, V("ZL", lo, hi), A.max)
        on, oc, oy, t1, t2 = (V(n, 0, h) for n in ("ON", "OC", "OY", "T1", "T2"))
        far = a + (FAR if L > 128 else FAR // 2)
        put_m = lambda: cp(ind(V("C", a, far), on), m)
        put_s = lambda: act(ind(V("SS", 16, 16 + far - a), on), sg, AF.Silu)

        def settle():
            act(V("SR"), V("SS", 16, 144), AF.Identity, bias=ROUND - LIFT)
            act(V("S", a, a + 128), V("SR"), AF.Identity, bias=-ROUND)

        def refill():
            iota(V("SS", 0, 160), [[0, 160]], int(LIFT))
        put_y = lambda: tt(ind(V("C", 0, a), oy), cg, m, A.subtract)

        def number():
            act(V("NR", 0, L), ind(V("TB"), oc), AF.Identity, bias=float(n0 - 4096))
        if e == 0:
            cp(on, V("LP", 16, 16 + h))
            tt(t1, V("LP", 32, 32 + h), yf, A.min)
            put_s()
            ts(oc, V("LP", 16, 16 + h), 128.0, A.min)
            tt(t2, t1, V("DUMP", 0, h), A.max)
            put_m()
            twice(a)
            counts(0, V("C", a, a + 128))
            settle()
            payload(0, V("S", a, a + 128))
            number()
            first()
            f1, f2, f3 = lists(("SS", 16), 128, [V("OKN")], [V("SEL", 0, 8)], LIFT)
            cp(oy, t2)
            f1()
            f2()
            put_y()
            f3()
            refill()
            zero(V("C", a + 128, a + 256))
        else:
            tt(t1, V("LP", 32, 32 + h), yf, A.min)
            cp(on, V("LP", 16, 16 + h))
            tt(t2, t1, V("DUMP", 0, h), A.max)
            ts(oc, V("LP", 16, 16 + h), 128.0, A.min)
            cp(oy, t2)
            number()
            first()
            if u == 5:
                put_s()
                settle()
                put_y()
                dma("sync", T.yc[:, 0:n0], T.C[:, PAD:a], [], [V("C", PAD, a)])
                put_m()
                dma("sync", T.yc[:, n0:NV], T.C[:, a:COL], [], [V("C", a, COL)])
                link()
                dma("sync", T.ys[:, 1088:1344], T.S[:, PAD + 2496:COL], [], [V("S", PAD + 2496, COL)])
                return
            put_y()
            twice(ent + 160)
            put_m()
            slot.extend([put_s, settle, refill])
        tail.append(link)
        if u == 4:
            tail.append(lambda: dma("sync", T.ys[:, 0:1088], T.S[:, PAD + 1408:PAD + 2496], [],
                                    [V("S", PAD + 1408, PAD + 2496)]))
        if e:
            nxt, prv = T.cores[(rank + 1) % len(T.cores)], T.cores[(rank - 1) % len(T.cores)]
            rid, pid = topo.addr(nxt)[:2]
            me, got = topo.engines(core, nxt)[:8], len(topo.engines(prv, core)[:8])
            src, dst = V("C", a, a + 96), V("P%d" % (t + 1), 32, 128)
            snd, arr = "snd%d" % (t + 1), "arr%d" % (t + 1)
            need("qp", [], [src])
            g.remote_dma(dst[0], src[0], T.sem[arr], T.sem[snd], pid, rid, sum(1 << i for i in me))
            note((snd, len(me)), [], [src])
            note((arr, got), [dst], [])

    for u in range(6):
        step(u)
    for s in range(dmas[0]):
        g.sync.wait_ge(T.sem[DSEMS[s]], 16)
    for q in QUEUES:
        g.sync.wait_ge(T.sem[q], cnt[q])
